import numpy as np, ml_dtypes
CORES = [3,7,11,15,131,135,139,143]
N = 8
BF = ml_dtypes.bfloat16
P, CB, W, RU, HB = 1792, 12, 4096, 4, 2
def step(x, inv, wa, kc, hi, lo):
    v = np.add.reduce(x * wa[..., None], axis=2); src = v >= hi[..., None]; blk = v <= lo[..., None]
    cl = np.add.reduce((x >= 128) * kc[..., None], axis=2)
    new = []
    for a in range(N):
        b = max(0, a - HB); L = (a - b + 1) * P; at = np.arange(L)
        s = np.concatenate(src[b:a + 1], axis=1); k = np.concatenate(cl[b:a + 1], axis=1)
        wall = np.maximum.accumulate(np.where(np.concatenate(blk[b:a + 1], axis=1), at, -1), axis=1)[:, L - P:]
        near = np.full((8, P), -1)
        for c in range(16):
            last = np.maximum.accumulate(np.where(s & (k == c), at, -1), axis=1)
            last = np.concatenate([np.full((8, 1), -1), last[:, :-1]], axis=1)[:, L - P:]
            near = np.where(cl[a] == c, last, near)
        ok = (near > wall) & ~blk[a]
        got = np.take_along_axis(np.concatenate(x[b:a + 1], axis=2), np.maximum(near, 0)[:, None, :], 2)
        new.append(np.where(ok[:, None, :] & (x[a] < 64), got, x[a]))
    x = np.stack(new)
    code = np.add.reduce((x[:, :, :CB] >= 128) * (1 << np.arange(CB))[:, None], axis=2)
    return (x + np.take_along_axis(inv, code[:, :, None, :], 3)) & 255
def parts(rng):
    x = rng.integers(0, 256, (N, 8, 16, P)); few = rng.choice(np.array([0.0, 0.2, 0.4]), (N, 8, 1, 1))
    x = np.where(rng.random(x.shape) < few, x >> 2, x); inv = rng.integers(0, 256, (N, 8, 16, W))
    wa = rng.integers(-3, 4, (N, 8, 16, RU)); wa[:, :, 0] = rng.choice(np.array([-3, -2, 2, 3]), (N, 8, RU))
    o = np.argsort(rng.random((N, 8, 16, RU)), axis=2); kc = np.where(o < 4, 1 << np.minimum(o, 3), 0)
    m = 127.5 * np.sum(wa, axis=2); s = 74.0 * np.sqrt(np.sum(wa * wa, axis=2))
    hi = np.floor(m + s * rng.choice(np.array([0.5, 1.0, 1.5, 3.0]), (N, 8, RU))).astype(np.int64)
    lo = np.floor(m - s * rng.choice(np.array([1.5, 2.0, 2.5, 9.0]), (N, 8, RU))).astype(np.int64)
    return x, inv, wa, kc, hi, lo
def pack(x, inv, wa, kc, hi, lo):
    return {"x": x.reshape(N, 128, P).astype(np.float32).astype(BF), "inv": inv.reshape(N, 128, W).astype(np.float32).astype(BF),
            "wa": wa.reshape(N, 128, RU).astype(np.float32).astype(BF), "kc": kc.reshape(N, 128, RU).astype(np.float32).astype(BF),
            "hl": np.repeat(np.concatenate([hi, lo], axis=2), 16, axis=1).astype(np.float32)}
def fit(x, inv, wa, kc, qh, ql):
    hi = np.zeros((N, 8, RU), np.int64); lo = np.zeros((N, 8, RU), np.int64)
    ih = (qh * (P - 1)).astype(np.int64)[..., None]; il = np.maximum(ql * (P - 1), 0).astype(np.int64)[..., None]
    for u in range(RU):
        v = np.sort(np.add.reduce(x * wa[..., u][..., None], axis=2), axis=-1)
        hi[..., u] = np.take_along_axis(v, ih, -1)[..., 0]
        lo[..., u] = np.minimum(np.where(ql < 0, v[..., 0] - 1, np.take_along_axis(v, il, -1)[..., 0]), hi[..., u] - 1)
        x = step(x, inv, wa[..., u], kc[..., u], hi[..., u], lo[..., u])
    return hi, lo
def staged(rng, x, inv, wa, kc, hi, lo, kind, kl):
    wa[..., 0] = 0; wa[:, :, 15, 0] = 3; kc[..., 0] = 0; hi[..., 0] = 738; lo[..., 0] = 27
    x[:, :, 15] = np.where(kind == 1, rng.integers(246, 256, kind.shape), np.where(kind == 2, rng.integers(0, 10, kind.shape), rng.integers(10, 246, kind.shape)))
    for i, w in enumerate((1, 6, 11, 14)):
        kc[:, :, w, 0] = 1 << i; x[:, :, w] = (x[:, :, w] & 127) + 128 * ((kl >> i) & 1)
    return pack(x, inv, wa, kc, hi, lo)
def setup_inputs(rng):
    return pack(*parts(rng))
def setup_inputs_full(rng):
    p = parts(rng); r = rng.random((N, 8, P)); kind = np.where(r < 0.05, 1, np.where(r < 0.055, 2, 0)); kl = rng.integers(0, 16, (N, 8, P))
    x, hi, lo = p[0], p[4], p[5]
    for q in range(N):
        for g in range(8):
            e = P - 16 - int(rng.integers(0, 48)); mode = g % 5 if q == 0 else int(rng.integers(0, 5))
            if mode == 2:
                kind[q, g] = np.where(kind[q, g] == 2, 0, kind[q, g]); kl[q, g] = np.where(kind[q, g] == 1, rng.integers(0, 16), kl[q, g])
            else:
                kind[q, g, e:] = 0; kind[q, g, e:e + 16] = 1; kl[q, g, e:e + 16] = rng.permutation(16)
                if mode == 1: kind[q, g, P - 1] = 2
                if mode == 3: kind[q, g, e - 1] = 2
                if mode == 4: kind[q, g, e + 8] = 2
            kind[q, g, :P // 2 if q == 1 else int(rng.choice(np.array([0, 1, 40, P // 2])))] = 0
    c = rng.permutation(16)
    kind[0, 2] = np.where(rng.random(P) < 0.97, 1, 0); kl[0, 2] = np.where(kind[0, 2] == 1, c[2], kl[0, 2])
    kind[:HB + 1, 7] = 1; kl[:HB + 1, 7] = c[0]; kl[0, 7, 1] = c[1]
    kind[HB, 7, P - 32:] = 0; kl[HB, 7, P - 32:] = c[1]
    x[:HB + 1, 7, 2:4] = x[:HB + 1, 7, 2:4] >> 2; x[HB, 7, 0, P - 32:] = x[HB, 7, 0, P - 32:] >> 2; x[0, 7, 0, 1] = 200
    hi[:2, 0, 1] = 16384; lo[:2, 0, 1] = -16384
    return staged(rng, *p, kind, kl)
def setup_inputs_ends(rng):
    p = parts(rng); kind = np.zeros((N, 8, P), np.int64); kl = rng.integers(0, 16, (N, 8, P)); some = (rng.random((N, 8, P)) < 0.05).astype(np.int64)
    g, h, j = rng.permutation(8)[:3]
    for q in range(N):
        o = np.concatenate([np.array([g]), rng.permutation(np.delete(np.arange(8), g))])
        kind[q, o[1], 0] = 1; kind[q, o[2], P - 1] = 1
        kind[q, o[3]] = some[q, o[3]]; kind[q, o[3], 0] = 2
        kind[q, o[4]] = 1; kind[q, o[5]] = 2
        kind[q, o[6], ::2] = 1; kind[q, o[6], 1::2] = 2
        kind[q, o[7]] = some[q, o[7]]; kind[q, o[7], P - 2] = 1; kind[q, o[7], P - 1] = 2
    kind[:, g] = 0; kind[0, g] = some[0, g]
    kind[:2, h] = 0; kind[0, h, 0] = 1; kind[:2, j] = 0; kind[0, j, P - 1] = 1
    return staged(rng, *p, kind, kl)
def setup_inputs_ties(rng):
    x, inv, wa, kc, hi, lo = parts(rng)
    x = np.where(rng.random(x.shape) < 0.5, rng.choice(np.array([0, 63, 64, 127, 128, 255]), x.shape), x)
    inv = np.where(rng.random(inv.shape) < 0.5, rng.choice(np.array([0, 1, 64, 128, 192, 255]), inv.shape), inv)
    ql = rng.choice(np.array([0.0, 0.03, 0.1, 0.85]), (N, 8)); ql[0, 0] = 0.85; ql[1, 0] = 0.03
    for g, w in ((2, 3), (3, -3)):
        wa[:, g, :, 0] = w; ql[:, g] = 0.03
        small = (kc[:, g, :, 0] == 0)[..., None] & (rng.random((N, 16, P)) < 0.15)
        x[:, g] = np.where(rng.random((N, 1, P)) < 0.2, 255, np.where(small, 0, 192) + (x[:, g] >> 2))
    hi, lo = fit(x, inv, wa, kc, np.full((N, 8), 0.85), ql)
    return pack(x, inv, wa, kc, hi, lo)
def setup_inputs_alike(rng):
    x, inv, wa, kc, hi, lo = parts(rng)
    pat = rng.choice(np.array([0, 63, 64, 128, 255]), (N, 8, 16, 6)); pat[..., 0] = 0; pat[..., 1] = 255; pat[:, :, 0, 2] = 64; pat[:, :, 1, 2] = 128
    x = np.take_along_axis(pat, rng.integers(0, 6, (N, 8, 1, P)), 3); inv[:, 1::2] = 0
    hi, lo = fit(x, inv, wa, kc, np.full((N, 8), 0.6), rng.choice(np.array([-1.0, 0.05]), (N, 8)))
    return pack(x, inv, wa, kc, hi, lo)
def setup_inputs_spread(rng):
    x, inv, wa, kc, hi, lo = parts(rng)
    x = np.floor(np.exp2(8 * rng.random((N, 8, 1, P))) * rng.random((N, 8, 16, P))).astype(np.int64)
    inv = np.where(rng.random((N, 8, 1, W)) < 0.5, np.floor(np.exp2(8 * rng.random((N, 8, 1, W))) * rng.random((N, 8, 16, W))).astype(np.int64), inv)
    wa = np.where(rng.random(wa.shape) < 0.6, 0, rng.choice(np.array([-3, -1, 1, 3]), wa.shape))
    hi, lo = fit(x, inv, wa, kc, rng.choice(np.array([0.5, 0.9, 0.99, 0.9995]), (N, 8)), rng.choice(np.array([-1.0, 0.0, 0.01, 0.1]), (N, 8)))
    return pack(x, inv, wa, kc, hi, lo)
def check_inputs(d):
    bad = []
    for k, lo, hi in (("x", 0, 255), ("inv", 0, 255), ("wa", -3, 3), ("kc", 0, 8), ("hl", -16384, 16384)):
        a = np.asarray(d[k]).astype(np.float32)
        if not np.all((a >= lo) & (a <= hi) & (a == np.floor(a))): bad.append("range of " + k)
    k = np.sort(np.asarray(d["kc"]).astype(np.float32).reshape(N, 8, 16, RU), axis=2)
    if not np.all(k == np.array([0] * 12 + [1, 2, 4, 8], np.float32)[:, None]): bad.append("class weights of kc")
    h = np.asarray(d["hl"]).astype(np.float32).reshape(N, 8, 16, 2 * RU)
    if not np.all(h == h[:, :, :1]): bad.append("rows of hl alike in a group")
    if not np.all(h[..., RU:] < h[..., :RU]): bad.append("lo under hi")
    return bad
def reference(x, inv, wa, kc, hl):
    z = x.astype(np.float32).astype(np.int32).reshape(N, 8, 16, P); tab = inv.astype(np.float32).astype(np.int32).reshape(N, 8, 16, W)
    w = wa.astype(np.float32).astype(np.int32).reshape(N, 8, 16, RU); k = kc.astype(np.float32).astype(np.int32).reshape(N, 8, 16, RU)
    h = hl.astype(np.int32).reshape(N, 8, 16, 2 * RU)[:, :, 0]
    for u in range(RU): z = step(z, tab, w[..., u], k[..., u], h[..., u], h[..., RU + u])
    return {"y": z.reshape(N, 128, P).astype(np.float32).astype(BF)}

@@ -1,0 +1,389 @@
+from concourse.bass import DstId, RemoteDMATransfer
+from concourse.mybir import AluOpType as A, AxisListType, ActivationFunctionType as F
+
+P, W, RU, HB = 1792, 4096, 4, 2
+OFF = 32
+CUT = [0, 448, 896, 1344, 1792]
+NC, KP = 4, P // 16
+DELTA, MAGIC = 1.0 / 2048, 49152.0
+ENG = {"Z": "SSSV", "BA": "SS", "X": "SSSS", "U": "SSSS", "CAP": "SSSS", "Q": "SVSV", "T": "VVVV"}
+TRIES = 1500
+ZB, SB, MB, QB, UB = (0, 1, 0, 1), (2, 2, 2, 2), (3, 3, 3, 3), (4, 5, 4, 5), (0, 1, 0, 1)
+H, B, S4 = "float16", "bfloat16", "float32"
+
+SCRATCH = {nm: ("sbuf", [128, n], d) for (nms, n, d) in (
+    ("xw", OFF + P, B), ("tab", W, B), ("was kcs", 8, B), ("hls", 8, S4), ("bb nl ba tg rr", P, B), ("inc cap", P + 8, B),
+    ("st", P + 8, H), ("zz zs", P, H), ("uu", P, S4), ("aa", P, H if "S" in ENG["T"] else S4), ("ix cx", KP, "uint16"),
+    ("sx so", 8, "uint16"), ("snd in1 in2", 32 * RU, B), ("hh", 16, B), ("pi", 2, "int32"), ("col", 40, S4), ("mi", 144, S4),
+    ("g16 bm", 128, S4), ("cc", KP, S4), ("colc", KP, H), ("jt", 16, S4), ("yy s16", 64, S4), ("ri", 64, "int32"),
+    ("wb e1 ek", 512, B), ("ib nb", 128, B), ("ih nh", 128, H), ("sz", 144, H), ("sS sV sn", 144, B), ("tw", 48, S4))
+    for nm in nms.split()}
+for _b in range(8):
+    SCRATCH["ps%d" % _b] = ("psum", [128, 512], S4)
+SEMAPHORES = (["eV", "eS", "eP", "eG", "lw", "lk", "lh", "lt", "out", "sent"] + ["arr%d" % u for u in range(RU)]
+              + ["lx%d" % c for c in range(NC)])
+
+COST = {"V": (70, 1.04), "S": (100, 1.04), "P": (40, 0.52), "G": (170, 2.1), "Y": (60, 0.0)}
+GATHER, HOP, FLIGHT = 1.56, 110, 3000
+ORDERS = {}
+
+
+def masks(T, topo, r):
+    dst = [d for d in range(r + 1, r + HB + 1) if d < len(T.cores)]
+    es = [topo.engines(T.cores[r], T.cores[d]) for d in dst]
+    if len(es) == 1:
+        es = [es[0][len(es[0]) // 2:]]
+    elif len(es) == 2:
+        if es[0] == es[1]:
+            n = len(es[0]) // 2
+            es = [es[0][:n], es[0][n:]]
+        elif len(es[0]) > len(es[1]):
+            es = [[e for e in es[0] if e not in es[1]], es[1]]
+        else:
+            es = [es[0], [e for e in es[1] if e not in es[0]]]
+    return list(zip(dst, es))
+
+
+def arrange(ops):
+    n = len(ops)
+    succ = [[] for k in range(n)]
+    for k, o in enumerate(ops):
+        for d, soft in o["deps"].items():
+            succ[d].append((k, 0 if soft else HOP + ops[d]["lat"]))
+        if o["after"] is not None:
+            succ[o["after"]].append((k, FLIGHT))
+    tail = [0.0] * n
+    for k in range(n - 1, -1, -1):
+        tail[k] = ops[k]["c"] + max([w + tail[j] for (j, w) in succ[k]] + [ops[k]["lat"]])
+    eng, cost = [o["e"] for o in ops], [o["c"] for o in ops]
+    left0 = [len(o["deps"]) + (o["after"] is not None) for o in ops]
+
+    def once(pri, look):
+        left = list(left0)
+        ready = {e: {} for e in COST}
+        for k in range(n):
+            if left[k] == 0:
+                ready[eng[k]][k] = 0.0
+        due, free, order, end = [0.0] * n, {e: 0.0 for e in COST}, [], 0.0
+        for step in range(n):
+            t, e = min((max(free[e], min(r.values())), e) for e, r in ready.items() if r)
+            k = max((j for j, v in ready[e].items() if v <= t + look), key=lambda j: pri[j])
+            t = max(free[e], ready[e].pop(k))
+            free[e] = t + cost[k]
+            end = max(end, free[e] + ops[k]["lat"])
+            order.append((k, t))
+            for (j, w) in succ[k]:
+                due[j] = max(due[j], free[e] + w)
+                left[j] -= 1
+                if left[j] == 0:
+                    ready[eng[j]][j] = due[j]
+        return end, order
+
+    same = [[j for j in range(n) if ops[j]["name"] == o["name"] and eng[j] == o["e"]] for o in ops]
+    best, pri, look, x = once(tail, 150), tail, 150, 12345
+    for it in range(TRIES):
+        new = list(pri)
+        for m in range(3):
+            x = (x * 1103515245 + 12345) % 2147483648
+            k = (x >> 8) % n
+            x = (x * 1103515245 + 12345) % 2147483648
+            for j in same[k]:
+                new[j] += ((x >> 8) % 6001) - 3000
+        lk = (60, 150, 300, 450)[(x >> 20) % 4] if it % 3 == 0 else look
+        got = once(new, lk)
+        if got[0] <= best[0]:
+            best, pri, look = got, new, lk
+    return best[1]
+
+
+def rank_program(g, core, T, topo):
+    rank = T.rank_of(core)
+    if rank is None:
+        return
+    Q = {"V": g.vector, "S": g.scalar, "P": g.tensor, "G": g, "Y": g.sync}
+    ops, touch = [], {}
+
+    def ap(r):
+        return T[r[0]][:, r[1]:r[2]:r[3]] if len(r) > 3 else T[r[0]][:, r[1]:r[2]]
+
+    def val(s):
+        return ap(s) if isinstance(s, tuple) else s
+
+    def op(e, fn, rd, wr, n, sem=None, pre=None, after=None, chain=False, lat=0, tag=None):
+        acc = [(r[0], 0, 512, True) if r[0].startswith("ps") else (r[0], r[1], r[2], False) for r in rd if isinstance(r, tuple)]
+        acc += [(r[0], 0, 512, True) if r[0].startswith("ps") else (r[0], r[1], r[2], True) for r in wr]
+        deps = {}
+        for a in acc:
+            for (k, b) in touch.get(a[0], []):
+                if (a[3] or b[3]) and a[1] < b[2] and b[1] < a[2]:
+                    deps[k] = deps.get(k, True) and chain and a[0].startswith("ps") and ops[k]["e"] == "P"
+        for a in acc:
+            old = touch.get(a[0], [])
+            if a[3]:
+                old = [(k, b) for (k, b) in old if not (a[1] <= b[1] and b[2] <= a[2])]
+            touch[a[0]] = old + [(len(ops), a)]
+        ops.append({"e": e, "fn": fn, "deps": deps, "c": COST[e][0] + COST[e][1] * n, "sem": sem, "pre": pre, "after": after,
+                    "lat": lat, "name": (tag or acc[-1][0]) + str(acc[-1 - (tag is not None)][1] // 440)})
+        return len(ops) - 1
+
+    def two(*rs):
+        return all(SCRATCH[r[0]][2] in (B, H) for r in rs)
+
+    def ts(o, i, s1, s2, o0, o1=None):
+        n = (o[2] - o[1]) * (0.5 if two(o, i) else 1)
+        if o1 is None:
+            return op("V", lambda q: q.tensor_scalar(ap(o), ap(i), val(s1), None, o0), [i, s1], [o], n)
+        return op("V", lambda q: q.tensor_scalar(ap(o), ap(i), val(s1), val(s2), o0, o1), [i, s1, s2], [o], n)
+
+    def tt(o, a, b, f, **k):
+        return op("V", lambda q: q.tensor_tensor(ap(o), ap(a), ap(b), f), [a, b], [o], 2 * (o[2] - o[1]), **k)
+
+    def cp(o, i, **k):
+        return op("V", lambda q: q.tensor_copy(ap(o), ap(i)), [i], [o], o[2] - o[1], **k)
+
+    def ms(o, v):
+        return op("V", lambda q: q.memset(ap(o), v), [], [o], o[2] - o[1])
+
+    def scan(o, d0, d1, ini, o0, o1):
+        return op("V", lambda q: q.tensor_tensor_scan(ap(o), ap(d0), ap(d1), val(ini), o0, o1), [d0, d1, ini], [o],
+                  (o[2] - o[1]) / 2)
+
+    def act(o, i, f, bias, scale):
+        return op("S", lambda q: q.activation(ap(o), ap(i), f, bias=val(bias), scale=val(scale)), [i, bias, scale], [o], o[2] - o[1])
+
+    def mm(o, pairs, start=True, stop=True):
+        def fn(q):
+            for k, (l, r) in enumerate(pairs):
+                last = q.matmul(ap(o), ap(l), ap(r), start and k == 0, stop and k == len(pairs) - 1)
+            return last
+        return op("P", fn, [x for p in pairs for x in p], [o], len(pairs) * max(64, o[2] - o[1]), chain=not start,
+                  tag=o[0] + pairs[-1][1][0])
+
+    def gat(o, win, off, other, f):
+        return op("V", lambda q: q.tensor_tensor(ap(o), ap(win).indirect(ap(off)), ap(other), f), [win, off, other], [o],
+                  GATHER * (o[2] - o[1]))
+
+    def iota(o, pat, base, cm):
+        if SCRATCH[o[0]][2] == "int32":
+            return op("G", lambda q: q.iota(ap(o), pat, base, cm), [], [o], o[2] - o[1])
+        return op("G", lambda q: q.iota(ap(o), pat, base, cm, allow_small_or_imprecise_dtypes=True), [], [o], o[2] - o[1])
+
+    def load(e, o, src, sem, lat):
+        k = op(e, lambda q: q.dma_start(ap(o), src), [], [o, ("turn" + e, 0, 1)], 0, sem=sem, lat=lat)
+        ops[k]["deps"] = {d: True for d in ops[k]["deps"]}
+
+    def C(k):
+        return ("col", k, k + 1)
+
+    def X(c):
+        return ("xw", OFF + CUT[c], OFF + CUT[c + 1])
+
+    def K(nm, c, sh=0, more=0):
+        return (nm, CUT[c] + sh, CUT[c + 1] + sh + more)
+
+    def PS(b, c):
+        return ("ps%d" % b, 0, CUT[c + 1] - CUT[c])
+
+    def KK(c, n=1):
+        return (CUT[c] // 16, CUT[c + n] // 16)
+
+    def fold(src, sel, h):
+        return [((sel, 15 - s, 143 - s), (src, CUT[2 * h] + s, CUT[2 * h + 2], 16)) for s in range(16)]
+
+    load("S", ("kcs", 0, 4), T.kc[:, :], "lk", 2200)
+    load("Y", X(0), T.x[:, CUT[0]:CUT[1]], "lx0", 2300)
+    load("Y", ("was", 0, 4), T.wa[:, :], "lw", 2200)
+    load("Y", ("hls", 0, 8), T.hl[:, :], "lh", 2200)
+    for c in range(1, NC):
+        load("Y", X(c), T.x[:, CUT[c]:CUT[c + 1]], "lx%d" % c, 2300 + 300 * c)
+    load("Y", ("tab", 0, W), T.inv[:, :], "lt", 7000)
+    iota(("pi", 0, 1), [[1, 1]], 0, 1)
+    iota(("mi", 0, 144), [[1, 144]], 0, 0)
+    iota(("g16", 0, 128), [[16, 8], [0, 16]], 0, 0)
+    iota(("cc", 0, KP), [[16, KP]], OFF - 2048, 0)
+    cp(C(0), ("pi", 0, 1))
+    ts(("pi", 1, 2), ("pi", 0, 1), 15, None, A.bitwise_and)
+    cp(C(1), ("pi", 1, 2))
+    tt(C(2), C(0), C(1), A.subtract)
+    ts(C(3), C(1), -DELTA, 15 * DELTA, A.mult, A.add)
+    ts(C(4), C(2), 15.0, None, A.add)
+    ts(("so", 0, 8), ("mi", 0, 8), 0.0, C(1), A.mult, A.add)
+    ts(("bm", 0, 128), ("g16", 0, 128), C(2), None, A.is_equal)
+    ts(("jt", 0, 16), ("mi", 0, 16), 0.5, None, A.add)
+    ts(("col", 8, 12), ("kcs", 0, 4), 0.5, 2.0, A.max, A.mult)
+    op("V", lambda q: q.reciprocal(ap(("col", 12, 16)), ap(("col", 8, 12))), [("col", 8, 12)], [("col", 12, 16)], 200)
+    cp(("col", 16, 20), ("kcs", 0, 4))
+    cp(("col", 32, 36), ("was", 0, 4))
+    ts(("col", 20, 24), ("hls", 0, 4), 65536.0, None, A.add)
+    for us in ((0,), (1, 2, 3)):
+        a = (16 * us[0], 16 * us[-1] + 16)
+        for u in us:
+            ts(("yy", 16 * u, 16 * u + 16), ("jt", 0, 16), C(12 + u), None, A.mult)
+        cp(("ri",) + a, ("yy",) + a)
+        tt(("yy",) + a, ("ri",) + a, ("yy",) + a, A.subtract)
+        for u in us:
+            b = (128 * u, 128 * u + 128)
+            act(("wb",) + b, ("bm", 0, 128), F.Identity, 0.0, C(32 + u))
+            act(("s16", 16 * u, 16 * u + 16), ("yy", 16 * u, 16 * u + 16), F.Sign, 0.0, C(16 + u))
+            gat(("e1",) + b, ("s16", 16 * u, 16 * u + 16), ("so", 0, 8), ("bm", 0, 128), A.mult)
+            act(("ek",) + b, ("e1",) + b, F.Identity, 0.0, 32768.0)
+    ms(("xw", 0, 16), -512.0)
+    ms(("cap", 0, 1), 2.0)
+    ms(("inc", P, P + 1), DELTA)
+    for nm, v in (("nh", -1.0), ("ib", 1.0), ("ih", 1.0), ("nb", -1.0)):
+        ts((nm, 0, 128), ("mi", 0, 128), C(0), v, A.is_equal, A.mult)
+    ts(("colc", 0, KP), ("cc", 0, KP), C(1), None, A.add)
+    ts(("sz", 0, 144), ("mi", 0, 144), C(4), 2048.0, A.is_equal, A.mult)
+    ms(("tw", 0, 12), 2.0)
+    ms(("tw", 12, 24), 0.0)
+    scan(("tw", 24, 36), ("tw", 0, 12), ("tw", 12, 24), 0.5, A.mult, A.add)
+    ts(("tw", 36, 48), ("mi", 0, 12), C(1), None, A.is_equal)
+    tt(("tw", 36, 48), ("tw", 36, 48), ("tw", 24, 36), A.mult)
+    op("V", lambda q: q.tensor_reduce(ap(C(6)), ap(("tw", 36, 48)), AxisListType.X, A.add), [("tw", 36, 48)], [C(6)], 12)
+    ts(("sV", 0, 144), ("mi", 0, 144), C(4), C(6), A.is_equal, A.mult)
+    act(("sS", 0, 144), ("sV", 0, 144), F.Identity, 0.0, 0.5)
+    act(("sn", 0, 144), ("sV", 0, 144), F.Identity, 0.0, -1.0 / 512)
+    for k, v in ((25, -1.0), (26, -256.0), (27, -127.5), (28, MAGIC), (29, MAGIC - 127.5)):
+        ms(C(k), v)
+
+    mine = masks(T, topo, rank)
+    come = [(d, len(es)) for d in range(1, HB + 1) if rank - d >= 0 for (t, es) in masks(T, topo, rank - d) if t == rank]
+
+    def evac(e, o, i, k, v, relu=False):
+        if e == "S":
+            return act(o, i, F.Relu if relu else F.Identity, C(k), 1.0)
+        return ts(o, i, v, 0.0, A.add, A.max) if relu else ts(o, i, v, None, A.add)
+
+    def bits(e, o, i):
+        if e == "S":
+            return act(o, i, F.Sign, C(27), 1.0)
+        return ts(o, i, 128.0, 0.5, A.is_ge, A.subtract)
+
+    def judge(u, c):
+        b = (128 * u, 128 * u + 128)
+        p0, p1 = PS(SB[c], c), PS(MB[c], c)
+        bits("V", K("bb", c), X(c))
+        mm(p0, [(("wb",) + b, X(c))])
+        ts(K("inc", c), p0, ("hls", 4 + u, 5 + u), DELTA, A.is_le, A.max)
+        mm(p1, [(("wb",) + b, X(c)), (("ek",) + b, K("bb", c))])
+        if ENG["CAP"][c] == "S":
+            act(K("cap", c, 1), p1, F.Relu, C(20 + u), -1.0)
+        else:
+            ts(K("cap", c, 1), p1, C(20 + u), None, A.is_lt)
+        m = 1 if c == NC - 1 else 0
+        ini = C(3) if c == 0 else ("st", CUT[c] - 1, CUT[c])
+        return scan(K("st", c, 0, m), K("cap", c, 0, m), K("inc", c, 0, m), ini, A.min, A.add)
+
+    def send(u):
+        s = ("snd", 32 * u, 32 * u + 32)
+        tr = []
+        for (t, es) in mine:
+            rid, pid = topo.addr(T.cores[t], core)
+            tr.append(RemoteDMATransfer(dst_ids=[DstId(rid=rid, pnc=pid)], dma_engine_mask=sum(1 << e for e in es),
+                                        remote_sem=T.sem["arr%d" % u], src=ap(s),
+                                        dst=ap(("in%d" % (t - rank), 32 * u, 32 * u + 32))))
+        return op("G", lambda q: q.remote_dma_fused(tr, local_sem=T.sem.sent), [s], [], 200, sem="")
+
+    def summary(u):
+        w, o, a = ("xw", 0, OFF + P), ("sx", 0, 1), 32 * u
+        ms(("xw", 16, 32), -1024.0)
+        ts(o, ("st", P, P + 1), -2048.0, float(OFF + P), A.mult, A.add)
+        op("V", lambda q: q.tensor_copy(ap(("snd", a, a + 16)), ap(w).indirect(ap(o))), [w, o], [("snd", a, a + 16)], 32)
+        op("V", lambda q: q.tensor_scalar(ap(("snd", a + 16, a + 32)), ap(w).indirect(ap(o)), 768.0, -4.0, A.add, A.mult),
+           [w, o], [("snd", a + 16, a + 32)], 32)
+        return send(u)
+
+    def tgather(c):
+        o, w, off = K("tg", c), ("tab", 0, W), ("cx",) + KK(c)
+        op("S", lambda q: q.activation(ap(o), ap(w).indirect(ap(off)), F.Identity), [w, off], [o], GATHER * (o[2] - o[1]))
+
+    def store(c):
+        op("Y", lambda q: q.dma_start(T.y[:, CUT[c]:CUT[c + 1]], ap(X(c))), [X(c)], [], 0, sem="out", lat=2500)
+
+    for c in range(NC):
+        last = judge(0, c)
+    for u in range(RU):
+        b = (128 * u, 128 * u + 128)
+        if mine:
+            last = summary(u)
+        for c in range(NC):
+            h = c // 2
+            pq, pu = PS(QB[c], c), PS(UB[c], c)
+            mm(pq, [(("e1",) + b, K("bb", c)), (("nh", 0, 128), K("st", c))])
+            evac(ENG["Z"][c], K("zz", c), pq, 25, -1.0, True)
+            ts(K("nl", c), X(c), 64.0, 512.0, A.is_ge, A.mult)
+            mm(pu, [(("ib", 0, 128), X(c)), (("ib", 0, 128), K("nl", c))])
+            evac(ENG["U"][c], K("uu", c), pu, 26, -256.0)
+            if c % 2:
+                kk = KK(c - 1, 2)
+                pk = ("ps%d" % (6 + h), 0, kk[1] - kk[0])
+                mm(pk, [(("ih", 0, 128), ("colc",) + kk)] + fold("zz", "sz", h))
+                cp(("ix",) + kk, pk)
+                mm(pk, fold("bb", "sV", h) + fold("nl", "sn", h), True, False)
+        slot, a = ("xw", 16, 32), 32 * u
+        arr = ("arr%d" % u, sum(n for (d, n) in come))
+        if len(come) == 1:
+            cp(slot, ("in1", a, a + 16), pre=arr, after=last)
+        elif len(come) == 2:
+            tt(("hh", 0, 16), ("in2", a, a + 16), ("in1", a + 16, a + 32), A.min, pre=arr, after=last)
+            tt(slot, ("in1", a, a + 16), ("hh", 0, 16), A.max)
+        for c in range(NC):
+            h = c // 2
+            gat(K("aa", c), ("xw", 0, OFF + CUT[c + 1]), ("ix",) + KK(c), K("uu", c), A.max)
+            bits(ENG["BA"][h], K("ba", c), K("aa", c))
+            if c % 2:
+                kk = KK(c - 1, 2)
+                pc = ("ps%d" % (6 + h), 0, kk[1] - kk[0])
+                mm(pc, fold("ba", "s" + ENG["BA"][h], h), False, True)
+                ts(("cx",) + kk, pc, 4095.0, None, A.add)
+        for c in range(NC):
+            pz = PS(ZB[c], c)
+            if ENG["T"][c] == "V":
+                gat(K("zs", c), ("tab", 0, W), ("cx",) + KK(c), K("aa", c), A.add)
+                evac(ENG["Q"][c], K("rr", c), K("zs", c), 29, MAGIC - 127.5)
+                mm(pz, [(("ih", 0, 128), K("zs", c)), (("nb", 0, 128), K("rr", c))])
+            else:
+                tgather(c)
+                pr = [(("ih", 0, 128), K("aa", c)), (("ib", 0, 128), K("tg", c))]
+                mm(PS(5, c), pr)
+                evac("S", K("rr", c), PS(5, c), 29, MAGIC - 127.5)
+                mm(pz, pr + [(("nb", 0, 128), K("rr", c))])
+            evac(ENG["X"][c], X(c), pz, 28, MAGIC)
+            if u + 1 < RU:
+                last = judge(u + 1, c)
+            else:
+                store(c)
+
+    kind = (len(mine) > 0, len(come))
+    if kind not in ORDERS:
+        ORDERS[kind] = arrange(ops)
+    count, mark, seen = {}, {}, {e: {} for e in Q}
+
+    def wait(e, s, v):
+        if seen[e].get(s, 0) < v:
+            Q[e].wait_ge(T.sem[s], v)
+            seen[e][s] = v
+
+    for (k, t) in ORDERS[kind]:
+        o = ops[k]
+        e = o["e"]
+        need = {}
+        for d, soft in o["deps"].items():
+            if not soft:
+                s, v = mark[d]
+                need[s] = max(need.get(s, 0), v)
+        for s, v in need.items():
+            wait(e, s, v)
+        if o["pre"]:
+            wait(e, *o["pre"])
+        ins = o["fn"](Q[e])
+        if o["sem"] != "":
+            s, v = (o["sem"], 16) if o["sem"] else ("e" + e, 1)
+            ins.then_inc(T.sem[s], v)
+            count[s] = count.get(s, 0) + v
+            mark[k] = (s, count[s])
+    if mine:
+        count["sent"] = sum(len(es) for (t, es) in mine) * RU
+    for s, v in count.items():
+        wait("G", s, v)
+    return [(ops[k]["e"], t, ops[k]["c"], ops[k]["name"]) for (k, t) in ORDERS[kind]]

@@ -6,25 +6,25 @@ OFF = 32
 CUT = [0, 448, 896, 1344, 1792]
 NC, KP = 4, P // 16
 DELTA, MAGIC = 1.0 / 2048, 49152.0
-ENG = {"Z": "SSSV", "BA": "SS", "X": "SSSS", "U": "SSSS", "CAP": "SSSS", "Q": "SVSV", "T": "VVVV"}
-TRIES = 1500
-ZB, SB, MB, QB, UB = (0, 1, 0, 1), (2, 2, 2, 2), (3, 3, 3, 3), (4, 5, 4, 5), (0, 1, 0, 1)
+ENG = {"Z": "SSSV", "X": "SSSS", "Q": "SSSV"}
+TRIES = 1200
+ZB, SB, MB, QB, UB = (0, 1, 0, 1), (2, 4, 2, 4), (3, 5, 3, 5), (6, 7, 6, 7), (0, 1, 0, 1)
 H, B, S4 = "float16", "bfloat16", "float32"
 
 SCRATCH = {nm: ("sbuf", [128, n], d) for (nms, n, d) in (
-    ("xw", OFF + P, B), ("tab", W, B), ("was kcs", 8, B), ("hls", 8, S4), ("bb nl ba tg rr", P, B), ("inc cap", P + 8, B),
-    ("st", P + 8, H), ("zz zs", P, H), ("uu", P, S4), ("aa", P, H if "S" in ENG["T"] else S4), ("ix cx", KP, "uint16"),
-    ("sx so", 8, "uint16"), ("snd in1 in2", 32 * RU, B), ("hh", 16, B), ("pi", 2, "int32"), ("col", 40, S4), ("mi", 144, S4),
-    ("g16 bm", 128, S4), ("cc", KP, S4), ("colc", KP, H), ("jt", 16, S4), ("yy s16", 64, S4), ("ri", 64, "int32"),
-    ("wb e1 ek", 512, B), ("ib nb", 128, B), ("ih nh", 128, H), ("sz", 144, H), ("sS sV sn", 144, B), ("tw", 48, S4))
+    ("xw", OFF + P, B), ("tab", W, B), ("was kcs", 8, B), ("hls", 8, S4), ("bb nl ba rr", P, B), ("inc cap", P + 8, B),
+    ("st", P + 8, H), ("zz zs", P, H), ("uu aa", P, S4), ("ix cx", KP, "uint16"),
+    ("sx", 8, "uint16"), ("snd in1 in2", 32 * RU, B), ("hh", 16, B), ("pi", 2, "int32"), ("col", 40, S4), ("mi", 144, S4),
+    ("g16 bm", 128, S4), ("cc", KP, S4), ("colc cb", KP, H), ("jt", 128, S4), ("yy", 512, S4),
+    ("wb e1 ek", 512, B), ("ib nb iw", 128, B), ("ih nh", 128, H), ("sz", 144, H), ("sS sV sn", 144, B), ("tw", 48, S4))
     for nm in nms.split()}
 for _b in range(8):
     SCRATCH["ps%d" % _b] = ("psum", [128, 512], S4)
 SEMAPHORES = (["eV", "eS", "eP", "eG", "lw", "lk", "lh", "lt", "out", "sent"] + ["arr%d" % u for u in range(RU)]
               + ["lx%d" % c for c in range(NC)])
 
-COST = {"V": (70, 1.04), "S": (100, 1.04), "P": (40, 0.52), "G": (170, 2.1), "Y": (60, 0.0)}
-GATHER, HOP, FLIGHT = 1.56, 110, 3000
+COST = {"V": (71.5, 1.079), "S": (169.0, 1.079), "P": (39.0, 0.546), "G": (170, 1.7), "Y": (60, 0.0)}
+GATHER, HOP, FLIGHT = 1.56, 140, 2800
 ORDERS = {}
 
 
@@ -109,14 +109,14 @@ def rank_program(g, core, T, topo):
     def val(s):
         return ap(s) if isinstance(s, tuple) else s
 
-    def op(e, fn, rd, wr, n, sem=None, pre=None, after=None, chain=False, lat=0, tag=None):
+    def op(e, fn, rd, wr, n, sem=None, pre=None, after=None, lat=0, tag=None):
         acc = [(r[0], 0, 512, True) if r[0].startswith("ps") else (r[0], r[1], r[2], False) for r in rd if isinstance(r, tuple)]
         acc += [(r[0], 0, 512, True) if r[0].startswith("ps") else (r[0], r[1], r[2], True) for r in wr]
         deps = {}
         for a in acc:
             for (k, b) in touch.get(a[0], []):
                 if (a[3] or b[3]) and a[1] < b[2] and b[1] < a[2]:
-                    deps[k] = deps.get(k, True) and chain and a[0].startswith("ps") and ops[k]["e"] == "P"
+                    deps[k] = False
         for a in acc:
             old = touch.get(a[0], [])
             if a[3]:
@@ -151,13 +151,12 @@ def rank_program(g, core, T, topo):
     def act(o, i, f, bias, scale):
         return op("S", lambda q: q.activation(ap(o), ap(i), f, bias=val(bias), scale=val(scale)), [i, bias, scale], [o], o[2] - o[1])
 
-    def mm(o, pairs, start=True, stop=True):
+    def mm(o, pairs):
         def fn(q):
             for k, (l, r) in enumerate(pairs):
-                last = q.matmul(ap(o), ap(l), ap(r), start and k == 0, stop and k == len(pairs) - 1)
+                last = q.matmul(ap(o), ap(l), ap(r), k == 0, k == len(pairs) - 1)
             return last
-        return op("P", fn, [x for p in pairs for x in p], [o], len(pairs) * max(64, o[2] - o[1]), chain=not start,
-                  tag=o[0] + pairs[-1][1][0])
+        return op("P", fn, [x for p in pairs for x in p], [o], len(pairs) * max(64, o[2] - o[1]), tag=o[0] + pairs[-1][1][0])
 
     def gat(o, win, off, other, f):
         return op("V", lambda q: q.tensor_tensor(ap(o), ap(win).indirect(ap(off)), ap(other), f), [win, off, other], [o],
@@ -187,8 +186,8 @@ def rank_program(g, core, T, topo):
     def KK(c, n=1):
         return (CUT[c] // 16, CUT[c + n] // 16)
 
-    def fold(src, sel, h):
-        return [((sel, 15 - s, 143 - s), (src, CUT[2 * h] + s, CUT[2 * h + 2], 16)) for s in range(16)]
+    def fold(src, sel, c0, c1):
+        return [((sel, 15 - s, 143 - s), (src, CUT[c0] + s, CUT[c1], 16)) for s in range(16)]
 
     load("S", ("kcs", 0, 4), T.kc[:, :], "lk", 2200)
     load("Y", X(0), T.x[:, CUT[0]:CUT[1]], "lx0", 2300)
@@ -207,30 +206,24 @@ def rank_program(g, core, T, topo):
     tt(C(2), C(0), C(1), A.subtract)
     ts(C(3), C(1), -DELTA, 15 * DELTA, A.mult, A.add)
     ts(C(4), C(2), 15.0, None, A.add)
-    ts(("so", 0, 8), ("mi", 0, 8), 0.0, C(1), A.mult, A.add)
+    ts(C(5), C(2), -0.5, None, A.add)
     ts(("bm", 0, 128), ("g16", 0, 128), C(2), None, A.is_equal)
-    ts(("jt", 0, 16), ("mi", 0, 16), 0.5, None, A.add)
-    ts(("col", 8, 12), ("kcs", 0, 4), 0.5, 2.0, A.max, A.mult)
-    op("V", lambda q: q.reciprocal(ap(("col", 12, 16)), ap(("col", 8, 12))), [("col", 8, 12)], [("col", 12, 16)], 200)
-    cp(("col", 16, 20), ("kcs", 0, 4))
-    cp(("col", 32, 36), ("was", 0, 4))
+    ts(("jt", 0, 128), ("mi", 0, 128), C(5), 1.0 / 16, A.subtract, A.mult)
+    tt(("jt", 0, 128), ("jt", 0, 128), ("bm", 0, 128), A.mult)
+    ts(("col", 32, 36), ("was", 0, 4), 1.0 / 32768, None, A.mult)
     ts(("col", 20, 24), ("hls", 0, 4), 65536.0, None, A.add)
-    for us in ((0,), (1, 2, 3)):
-        a = (16 * us[0], 16 * us[-1] + 16)
-        for u in us:
-            ts(("yy", 16 * u, 16 * u + 16), ("jt", 0, 16), C(12 + u), None, A.mult)
-        cp(("ri",) + a, ("yy",) + a)
-        tt(("yy",) + a, ("ri",) + a, ("yy",) + a, A.subtract)
-        for u in us:
-            b = (128 * u, 128 * u + 128)
-            act(("wb",) + b, ("bm", 0, 128), F.Identity, 0.0, C(32 + u))
-            act(("s16", 16 * u, 16 * u + 16), ("yy", 16 * u, 16 * u + 16), F.Sign, 0.0, C(16 + u))
-            gat(("e1",) + b, ("s16", 16 * u, 16 * u + 16), ("so", 0, 8), ("bm", 0, 128), A.mult)
-            act(("ek",) + b, ("e1",) + b, F.Identity, 0.0, 32768.0)
+    ts(("col", 8, 12), ("hls", 4, 8), 1.0 / 32768, None, A.mult)
+    for u in range(RU):
+        b = (128 * u, 128 * u + 128)
+        act(("wb",) + b, ("bm", 0, 128), F.Identity, 0.0, C(32 + u))
+        ts(("ek",) + b, ("jt", 0, 128), ("kcs", u, u + 1), 192.0, A.mult, A.add)
+        ts(("yy",) + b, ("jt", 0, 128), ("kcs", u, u + 1), 192.0, A.mult, A.add)
+        tt(("yy",) + b, ("ek",) + b, ("yy",) + b, A.subtract)
+        act(("e1",) + b, ("yy",) + b, F.Sign, 0.0, 1.0)
     ms(("xw", 0, 16), -512.0)
     ms(("cap", 0, 1), 2.0)
     ms(("inc", P, P + 1), DELTA)
-    for nm, v in (("nh", -1.0), ("ib", 1.0), ("ih", 1.0), ("nb", -1.0)):
+    for nm, v in (("nh", -1.0), ("ib", 1.0), ("ih", 1.0), ("nb", -1.0), ("iw", 512.0)):
         ts((nm, 0, 128), ("mi", 0, 128), C(0), v, A.is_equal, A.mult)
     ts(("colc", 0, KP), ("cc", 0, KP), C(1), None, A.add)
     ts(("sz", 0, 144), ("mi", 0, 144), C(4), 2048.0, A.is_equal, A.mult)
@@ -242,8 +235,8 @@ def rank_program(g, core, T, topo):
     op("V", lambda q: q.tensor_reduce(ap(C(6)), ap(("tw", 36, 48)), AxisListType.X, A.add), [("tw", 36, 48)], [C(6)], 12)
     ts(("sV", 0, 144), ("mi", 0, 144), C(4), C(6), A.is_equal, A.mult)
     act(("sS", 0, 144), ("sV", 0, 144), F.Identity, 0.0, 0.5)
-    act(("sn", 0, 144), ("sV", 0, 144), F.Identity, 0.0, -1.0 / 512)
-    for k, v in ((25, -1.0), (26, -256.0), (27, -127.5), (28, MAGIC), (29, MAGIC - 127.5)):
+    act(("sn", 0, 144), ("sV", 0, 144), F.Identity, 0.0, -1.0)
+    for k, v in ((25, -1.0), (36, 2048.0), (27, -127.5), (28, MAGIC), (29, MAGIC - 127.5)):
         ms(C(k), v)
 
     mine = masks(T, topo, rank)
@@ -254,22 +247,14 @@ def rank_program(g, core, T, topo):
             return act(o, i, F.Relu if relu else F.Identity, C(k), 1.0)
         return ts(o, i, v, 0.0, A.add, A.max) if relu else ts(o, i, v, None, A.add)
 
-    def bits(e, o, i):
-        if e == "S":
-            return act(o, i, F.Sign, C(27), 1.0)
-        return ts(o, i, 128.0, 0.5, A.is_ge, A.subtract)
-
     def judge(u, c):
         b = (128 * u, 128 * u + 128)
         p0, p1 = PS(SB[c], c), PS(MB[c], c)
-        bits("V", K("bb", c), X(c))
+        ts(K("bb", c), X(c), 128.0, 0.5, A.is_ge, A.subtract)
         mm(p0, [(("wb",) + b, X(c))])
-        ts(K("inc", c), p0, ("hls", 4 + u, 5 + u), DELTA, A.is_le, A.max)
-        mm(p1, [(("wb",) + b, X(c)), (("ek",) + b, K("bb", c))])
-        if ENG["CAP"][c] == "S":
-            act(K("cap", c, 1), p1, F.Relu, C(20 + u), -1.0)
-        else:
-            ts(K("cap", c, 1), p1, C(20 + u), None, A.is_lt)
+        ts(K("inc", c), p0, C(8 + u), DELTA, A.is_le, A.max)
+        mm(p1, [(("wb",) + b, X(c)), (("e1",) + b, K("bb", c))])
+        act(K("cap", c, 1), p1, F.Relu, C(20 + u), -32768.0)
         m = 1 if c == NC - 1 else 0
         ini = C(3) if c == 0 else ("st", CUT[c] - 1, CUT[c])
         return scan(K("st", c, 0, m), K("cap", c, 0, m), K("inc", c, 0, m), ini, A.min, A.add)
@@ -293,10 +278,6 @@ def rank_program(g, core, T, topo):
            [w, o], [("snd", a + 16, a + 32)], 32)
         return send(u)
 
-    def tgather(c):
-        o, w, off = K("tg", c), ("tab", 0, W), ("cx",) + KK(c)
-        op("S", lambda q: q.activation(ap(o), ap(w).indirect(ap(off)), F.Identity), [w, off], [o], GATHER * (o[2] - o[1]))
-
     def store(c):
         op("Y", lambda q: q.dma_start(T.y[:, CUT[c]:CUT[c + 1]], ap(X(c))), [X(c)], [], 0, sem="out", lat=2500)
 
@@ -307,19 +288,16 @@ def rank_program(g, core, T, topo):
         if mine:
             last = summary(u)
         for c in range(NC):
-            h = c // 2
             pq, pu = PS(QB[c], c), PS(UB[c], c)
             mm(pq, [(("e1",) + b, K("bb", c)), (("nh", 0, 128), K("st", c))])
             evac(ENG["Z"][c], K("zz", c), pq, 25, -1.0, True)
-            ts(K("nl", c), X(c), 64.0, 512.0, A.is_ge, A.mult)
-            mm(pu, [(("ib", 0, 128), X(c)), (("ib", 0, 128), K("nl", c))])
-            evac(ENG["U"][c], K("uu", c), pu, 26, -256.0)
-            if c % 2:
-                kk = KK(c - 1, 2)
-                pk = ("ps%d" % (6 + h), 0, kk[1] - kk[0])
-                mm(pk, [(("ih", 0, 128), ("colc",) + kk)] + fold("zz", "sz", h))
-                cp(("ix",) + kk, pk)
-                mm(pk, fold("bb", "sV", h) + fold("nl", "sn", h), True, False)
+            ts(K("nl", c), X(c), 64.0, 0.5, A.is_ge, A.subtract)
+            mm(pu, [(("ib", 0, 128), X(c)), (("iw", 0, 128), K("nl", c))])
+            act(K("uu", c), pu, F.Identity, 0.0, 1.0)
+        mm(("ps2", 0, KP), [(("ih", 0, 128), ("colc", 0, KP))] + fold("zz", "sz", 0, NC))
+        cp(("ix", 0, KP), ("ps2", 0, KP))
+        mm(("ps7", 0, KP), fold("bb", "sV", 0, NC) + fold("nl", "sn", 0, NC))
+        evac("S", ("cb", 0, KP), ("ps7", 0, KP), 36, 2048.0)
         slot, a = ("xw", 16, 32), 32 * u
         arr = ("arr%d" % u, sum(n for (d, n) in come))
         if len(come) == 1:
@@ -328,26 +306,18 @@ def rank_program(g, core, T, topo):
             tt(("hh", 0, 16), ("in2", a, a + 16), ("in1", a + 16, a + 32), A.min, pre=arr, after=last)
             tt(slot, ("in1", a, a + 16), ("hh", 0, 16), A.max)
         for c in range(NC):
-            h = c // 2
             gat(K("aa", c), ("xw", 0, OFF + CUT[c + 1]), ("ix",) + KK(c), K("uu", c), A.max)
-            bits(ENG["BA"][h], K("ba", c), K("aa", c))
+            act(K("ba", c), K("aa", c), F.Sign, C(27), 1.0)
             if c % 2:
                 kk = KK(c - 1, 2)
-                pc = ("ps%d" % (6 + h), 0, kk[1] - kk[0])
-                mm(pc, fold("ba", "s" + ENG["BA"][h], h), False, True)
-                ts(("cx",) + kk, pc, 4095.0, None, A.add)
+                pc = ("ps%d" % (6 + c // 2), 0, kk[1] - kk[0])
+                mm(pc, [(("ih", 0, 128), ("cb",) + kk)] + fold("ba", "sS", c - 1, c + 1))
+                ts(("cx",) + kk, pc, -0.5, None, A.add)
         for c in range(NC):
             pz = PS(ZB[c], c)
-            if ENG["T"][c] == "V":
-                gat(K("zs", c), ("tab", 0, W), ("cx",) + KK(c), K("aa", c), A.add)
-                evac(ENG["Q"][c], K("rr", c), K("zs", c), 29, MAGIC - 127.5)
-                mm(pz, [(("ih", 0, 128), K("zs", c)), (("nb", 0, 128), K("rr", c))])
-            else:
-                tgather(c)
-                pr = [(("ih", 0, 128), K("aa", c)), (("ib", 0, 128), K("tg", c))]
-                mm(PS(5, c), pr)
-                evac("S", K("rr", c), PS(5, c), 29, MAGIC - 127.5)
-                mm(pz, pr + [(("nb", 0, 128), K("rr", c))])
+            gat(K("zs", c), ("tab", 0, W), ("cx",) + KK(c), K("aa", c), A.add)
+            evac(ENG["Q"][c], K("rr", c), K("zs", c), 29, MAGIC - 127.5)
+            mm(pz, [(("ih", 0, 128), K("zs", c)), (("nb", 0, 128), K("rr", c))])
             evac(ENG["X"][c], X(c), pz, 28, MAGIC)
             if u + 1 < RU:
                 last = judge(u + 1, c)

@@ -2,29 +2,36 @@ from concourse.bass import DstId, RemoteDMATransfer
 from concourse.mybir import AluOpType as A, AxisListType, ActivationFunctionType as F
 
 P, W, RU, HB = 1792, 4096, 4, 2
-OFF = 32
-CUT = [0, 448, 896, 1344, 1792]
-NC, KP = 4, P // 16
-DELTA, MAGIC = 1.0 / 2048, 49152.0
-ENG = {"Z": "SSSV", "X": "SSSS", "Q": "SSSV"}
-TRIES = 1200
-ZB, SB, MB, QB, UB = (0, 1, 0, 1), (2, 4, 2, 4), (3, 5, 3, 5), (6, 7, 6, 7), (0, 1, 0, 1)
+Q, OFF, WIN = P // 2, 96, 992
+CUT = [0, 480, 896]
+NC, KP = 2, Q // 16
+DELTA, BAND, GRID, WIDE = 1.0 / 1024, 3.0 * 2 ** 27 + 32, 3.0 * 2 ** 27, 3.0 * 2 ** 30
+NONE, OPEN, NK = -16384, -32768, 5
+ENG = {"Z": "SS", "Q": "SS", "U": "S", "T": "SS", "C": "S", "B": "S"}
+LAST = {("T", 3, 1): "SV", ("Q", 3, 1): "SV"}
+TRIES = 6000
 H, B, S4 = "float16", "bfloat16", "float32"
 
 SCRATCH = {nm: ("sbuf", [128, n], d) for (nms, n, d) in (
-    ("xw", OFF + P, B), ("tab", W, B), ("was kcs", 8, B), ("hls", 8, S4), ("bb nl ba rr", P, B), ("inc cap", P + 8, B),
-    ("st", P + 8, H), ("zz zs", P, H), ("uu aa", P, S4), ("ix cx", KP, "uint16"),
-    ("sx", 8, "uint16"), ("snd in1 in2", 32 * RU, B), ("hh", 16, B), ("pi", 2, "int32"), ("col", 40, S4), ("mi", 144, S4),
-    ("g16 bm", 128, S4), ("cc", KP, S4), ("colc cb", KP, H), ("jt", 128, S4), ("yy", 512, S4),
-    ("wb e1 ek", 512, B), ("ib nb iw", 128, B), ("ih nh", 128, H), ("sz", 144, H), ("sS sV sn", 144, B), ("tw", 48, S4))
+    ("xw0 xw1", WIN, B), ("tab0 tab1", W, B), ("was kcs", 32, B), ("hls hi lo", 32, S4),
+    ("bb0 bb1 zs0 zs1 ba0 ba1 rr0 rr1", Q, B), ("cap0 cap1", Q + 8, B), ("inc0 inc1 st0 st1", Q + 8, H),
+    ("zz0 zz1 gr0 gr1 uu0 uu1 aa0 aa1", Q, H), ("ix0 ix1 cx0 cx1", KP, "uint16"), ("sx0 sx1", 4, "uint16"),
+    ("snd in1 in2", 16 * 2 * RU, B),
+    ("pi", 32, "int32"), ("of", 24, "uint16"), ("col", 16, S4), ("mi", 144, S4), ("g16 jt yy ek", 128, S4),
+    ("cc", KP, S4), ("colc cb0 cb1", KP, H), ("cw", 256, B), ("bm b64 ib sh ns up dn lu nd no", 128, B), ("ih nh ir i4 r4", 128, H),
+    ("sz", 144, H), ("sv", 144, B), ("kt rs", 80, B), ("tw", 72, S4), ("ew", 2048, B))
     for nm in nms.split()}
 for _b in range(8):
     SCRATCH["ps%d" % _b] = ("psum", [128, 512], S4)
-SEMAPHORES = (["eV", "eS", "eP", "eG", "lw", "lk", "lh", "lt", "out", "sent"] + ["arr%d" % u for u in range(RU)]
-              + ["lx%d" % c for c in range(NC)])
+SEMAPHORES = (["eV", "eS", "eP", "eG", "lw0", "lk0", "lh0", "lw1", "lk1", "lh1", "lt0", "lt1", "out", "sent", "sent0", "sent1"]
+              + ["arr%d" % k for k in range(2 * RU)] + ["lx%d" % c for c in range(2 * NC)])
 
-COST = {"V": (71.5, 1.079), "S": (169.0, 1.079), "P": (39.0, 0.546), "G": (170, 1.7), "Y": (60, 0.0)}
-GATHER, HOP, FLIGHT = 1.56, 140, 2800
+FAC = 1.08
+COST = {"V": (55 * FAC, 0.83 * FAC), "S": (130 * FAC, 0.83 * FAC), "P": (30 * FAC, 0.42 * FAC), "G": (150 * FAC, 1.66 * FAC), "Y": (60, 0.0)}
+GATHER, HOP, FLIGHT, LAG, SEED = 1.56, 140, 3550, 3000, 123
+CF = True
+SPLIT = 2
+HEAT = 150
 ORDERS = {}
 
 
@@ -37,81 +44,121 @@ def masks(T, topo, r):
         if es[0] == es[1]:
             n = len(es[0]) // 2
             es = [es[0][:n], es[0][n:]]
-        elif len(es[0]) > len(es[1]):
-            es = [[e for e in es[0] if e not in es[1]], es[1]]
         else:
-            es = [es[0], [e for e in es[1] if e not in es[0]]]
+            (a, b) = (0, 1) if len(es[0]) > len(es[1]) else (1, 0)
+            es[a] = [e for e in es[a] if e not in es[b]]
+            es = [e[:len(e) // SPLIT] for e in es]
     return list(zip(dst, es))
 
 
 def arrange(ops):
     n = len(ops)
-    succ = [[] for k in range(n)]
-    for k, o in enumerate(ops):
-        for d, soft in o["deps"].items():
-            succ[d].append((k, 0 if soft else HOP + ops[d]["lat"]))
-        if o["after"] is not None:
-            succ[o["after"]].append((k, FLIGHT))
+    eng, cost, acc, lat = [o["e"] for o in ops], [o["c"] for o in ops], [o["acc"] for o in ops], [o["lat"] for o in ops]
+    edges = [(d, k, 0 if soft else HOP + lat[d]) for k, o in enumerate(ops) for d, soft in o["deps"].items()]
+    edges += [(o["after"], k, FLIGHT) for k, o in enumerate(ops) if o["after"] is not None]
+    users = {}
+    for k in range(n):
+        if acc[k]:
+            users.setdefault(acc[k], []).append(k)
+
+    def place(pri, nxt, cnt, first):
+        left, due, at = list(cnt), list(first), [0.0] * n
+        busy = {e: [] for e in COST}
+        ready = sorted((-pri[k], k) for k in range(n) if not left[k])
+        while ready:
+            k = ready.pop()[1]
+            t, c, b = due[k], cost[k], busy[eng[k]]
+            i = len(b)
+            while i and b[i - 1][1] > t:
+                i -= 1
+            while i < len(b) and b[i][0] < t + c:
+                t = max(t, b[i][1])
+                i += 1
+            b.insert(i, (t, t + c))
+            at[k] = t
+            for (j, w) in nxt[k]:
+                due[j] = max(due[j], t + c + w)
+                left[j] -= 1
+                if not left[j]:
+                    ready.append((-pri[j], j))
+                    ready.sort()
+        return at
+
+    def graph(es):
+        fw, bw = [[] for k in range(n)], [[] for k in range(n)]
+        for (a, b, w) in es:
+            fw[a].append((b, w))
+            bw[b].append((a, w))
+        return fw, bw, [len(v) for v in bw], [len(v) for v in fw]
+
+    def banks(at):
+        idle, bank = {b: (-1.0, None) for b in range(8)}, {}
+        for (t, a) in sorted((at[v[0]], a) for a, v in users.items()):
+            b = min(idle, key=lambda b: idle[b][0])
+            if idle[b][0] > t:
+                return None, (idle[b][1], users[a][0], HOP)
+            bank[a] = b
+            k = users[a][-1]
+            idle[b] = (at[k] + cost[k] + HOP, k)
+        return bank, None
+
+    def solve(pri, rounds):
+        best, extra, g = None, [], plain
+        for r in range(rounds):
+            while True:
+                at = place(pri, g[0], g[2], [0.0] * n)
+                bank, e = banks(at)
+                if bank:
+                    break
+                extra.append(e)
+                g = graph(edges + extra)
+            end = max(at[k] + cost[k] + lat[k] for k in range(n))
+            if best is not None and end >= best[0]:
+                break
+            best = (end, at, bank)
+            back = place([-(at[k] + cost[k]) for k in range(n)], g[1], g[3], lat)
+            pri = [-(back[k] + cost[k]) for k in range(n)]
+        return best
+
+    plain = graph(edges)
     tail = [0.0] * n
     for k in range(n - 1, -1, -1):
-        tail[k] = ops[k]["c"] + max([w + tail[j] for (j, w) in succ[k]] + [ops[k]["lat"]])
-    eng, cost = [o["e"] for o in ops], [o["c"] for o in ops]
-    left0 = [len(o["deps"]) + (o["after"] is not None) for o in ops]
-
-    def once(pri, look):
-        left = list(left0)
-        ready = {e: {} for e in COST}
-        for k in range(n):
-            if left[k] == 0:
-                ready[eng[k]][k] = 0.0
-        due, free, order, end = [0.0] * n, {e: 0.0 for e in COST}, [], 0.0
-        for step in range(n):
-            t, e = min((max(free[e], min(r.values())), e) for e, r in ready.items() if r)
-            k = max((j for j, v in ready[e].items() if v <= t + look), key=lambda j: pri[j])
-            t = max(free[e], ready[e].pop(k))
-            free[e] = t + cost[k]
-            end = max(end, free[e] + ops[k]["lat"])
-            order.append((k, t))
-            for (j, w) in succ[k]:
-                due[j] = max(due[j], free[e] + w)
-                left[j] -= 1
-                if left[j] == 0:
-                    ready[eng[j]][j] = due[j]
-        return end, order
-
-    same = [[j for j in range(n) if ops[j]["name"] == o["name"] and eng[j] == o["e"]] for o in ops]
-    best, pri, look, x = once(tail, 150), tail, 150, 12345
+        tail[k] = cost[k] + max([w + tail[j] for (j, w) in plain[0][k]] + [lat[k]])
+    best = solve([LAG * ops[k]["set"] - tail[k] for k in range(n)], 8)
+    x, cur = SEED, best
     for it in range(TRIES):
-        new = list(pri)
-        for m in range(3):
-            x = (x * 1103515245 + 12345) % 2147483648
-            k = (x >> 8) % n
-            x = (x * 1103515245 + 12345) % 2147483648
-            for j in same[k]:
-                new[j] += ((x >> 8) % 6001) - 3000
-        lk = (60, 150, 300, 450)[(x >> 20) % 4] if it % 3 == 0 else look
-        got = once(new, lk)
-        if got[0] <= best[0]:
-            best, pri, look = got, new, lk
-    return best[1]
+        x = (x * 1103515245 + 12345) % 2147483648
+        t0, pri, lag = cur[0] * ((x >> 8) % 1000) / 1000.0 - 2000, list(cur[1]), ((x >> 20) % 5 - 2) * 400
+        span, amp = (1500, 4000, 9000)[(x >> 12) % 3], (500, 1000, 2000)[(x >> 16) % 3]
+        for k in range(n):
+            if t0 <= pri[k] <= t0 + span:
+                x = (x * 1103515245 + 12345) % 2147483648
+                pri[k] += (x >> 8) % amp - amp / 2 + lag * ops[k]["set"]
+        got = solve(pri, 3)
+        if got[0] <= cur[0] + HEAT * (1 - it / TRIES) * ((x >> 5) % 8) / 8:
+            cur = got
+            if got[0] < best[0]:
+                best = got
+    return sorted(((k, best[1][k]) for k in range(n)), key=lambda v: (v[1], v[0])), best[2], users
 
 
 def rank_program(g, core, T, topo):
     rank = T.rank_of(core)
     if rank is None:
         return
-    Q = {"V": g.vector, "S": g.scalar, "P": g.tensor, "G": g, "Y": g.sync}
-    ops, touch = [], {}
+    QS = {"V": g.vector, "S": g.scalar, "P": g.tensor, "G": g, "Y": g.sync}
+    ops, touch, bank, fresh, now = [], {}, {}, [0], [0]
 
-    def ap(r):
-        return T[r[0]][:, r[1]:r[2]:r[3]] if len(r) > 3 else T[r[0]][:, r[1]:r[2]]
+    def ap(r, lo=0, hi=128):
+        t = T["ps%d" % bank[r[0]]] if r[0][0] == "@" else T[r[0]]
+        return t[lo:hi, r[1]:r[2]:r[3]] if len(r) > 3 else t[lo:hi, r[1]:r[2]]
 
     def val(s):
         return ap(s) if isinstance(s, tuple) else s
 
     def op(e, fn, rd, wr, n, sem=None, pre=None, after=None, lat=0, tag=None):
-        acc = [(r[0], 0, 512, True) if r[0].startswith("ps") else (r[0], r[1], r[2], False) for r in rd if isinstance(r, tuple)]
-        acc += [(r[0], 0, 512, True) if r[0].startswith("ps") else (r[0], r[1], r[2], True) for r in wr]
+        acc = [(r[0], 0, 512, True) if r[0][0] == "@" else (r[0], r[1], r[2], False) for r in rd if isinstance(r, tuple)]
+        acc += [(r[0], 0, 512, True) if r[0][0] == "@" else (r[0], r[1], r[2], True) for r in wr]
         deps = {}
         for a in acc:
             for (k, b) in touch.get(a[0], []):
@@ -122,12 +169,18 @@ def rank_program(g, core, T, topo):
             if a[3]:
                 old = [(k, b) for (k, b) in old if not (a[1] <= b[1] and b[2] <= a[2])]
             touch[a[0]] = old + [(len(ops), a)]
-        ops.append({"e": e, "fn": fn, "deps": deps, "c": COST[e][0] + COST[e][1] * n, "sem": sem, "pre": pre, "after": after,
-                    "lat": lat, "name": (tag or acc[-1][0]) + str(acc[-1 - (tag is not None)][1] // 440)})
+        ps = [a[0] for a in acc if a[0][0] == "@"]
+        ops.append({"e": e, "fn": fn, "deps": deps, "c": COST[e][0] + COST[e][1] * n, "n": n, "sem": sem, "pre": pre,
+                    "after": after, "lat": lat, "set": now[0], "acc": ps[0] if ps else None,
+                    "name": (tag or acc[-1][0]) + "." + str(acc[-1 - (tag is not None)][1] // 440)})
         return len(ops) - 1
 
+    def PS(n):
+        fresh[0] += 1
+        return ("@%d" % fresh[0], 0, n)
+
     def two(*rs):
-        return all(SCRATCH[r[0]][2] in (B, H) for r in rs)
+        return all(r[0] == "ew" or (r[0][0] != "@" and SCRATCH[r[0]][2] in (B, H)) for r in rs)
 
     def ts(o, i, s1, s2, o0, o1=None):
         n = (o[2] - o[1]) * (0.5 if two(o, i) else 1)
@@ -136,7 +189,8 @@ def rank_program(g, core, T, topo):
         return op("V", lambda q: q.tensor_scalar(ap(o), ap(i), val(s1), val(s2), o0, o1), [i, s1, s2], [o], n)
 
     def tt(o, a, b, f, **k):
-        return op("V", lambda q: q.tensor_tensor(ap(o), ap(a), ap(b), f), [a, b], [o], 2 * (o[2] - o[1]), **k)
+        return op("V", lambda q: q.tensor_tensor(ap(o), ap(a), ap(b), f), [a, b], [o],
+                  (1 if a[0][0] == "@" else 2) * (o[2] - o[1]), **k)
 
     def cp(o, i, **k):
         return op("V", lambda q: q.tensor_copy(ap(o), ap(i)), [i], [o], o[2] - o[1], **k)
@@ -144,216 +198,329 @@ def rank_program(g, core, T, topo):
     def ms(o, v):
         return op("V", lambda q: q.memset(ap(o), v), [], [o], o[2] - o[1])
 
+    def red(o, i, **k):
+        return op("V", lambda q: q.tensor_reduce(ap(o), ap(i), AxisListType.X, A.add, **k), [i], [o], i[2] - i[1])
+
     def scan(o, d0, d1, ini, o0, o1):
         return op("V", lambda q: q.tensor_tensor_scan(ap(o), ap(d0), ap(d1), val(ini), o0, o1), [d0, d1, ini], [o],
-                  (o[2] - o[1]) / 2)
+                  (o[2] - o[1]) * (0.5 if two(o, d0, d1) else 1))
 
     def act(o, i, f, bias, scale):
         return op("S", lambda q: q.activation(ap(o), ap(i), f, bias=val(bias), scale=val(scale)), [i, bias, scale], [o], o[2] - o[1])
 
-    def mm(o, pairs):
+    def mm(o, pairs, start=True, stop=True):
         def fn(q):
             for k, (l, r) in enumerate(pairs):
-                last = q.matmul(ap(o), ap(l), ap(r), k == 0, k == len(pairs) - 1)
+                last = q.matmul(ap(o), ap(l), ap(r), start and k == 0, stop and k == len(pairs) - 1)
             return last
-        return op("P", fn, [x for p in pairs for x in p], [o], len(pairs) * max(64, o[2] - o[1]), tag=o[0] + pairs[-1][1][0])
+        return op("P", fn, [x for p in pairs for x in p], [o], len(pairs) * max(64, o[2] - o[1]), tag="mm" + pairs[-1][1][0])
+
+    def sub(every, start, stop, use=None, **k):
+        terms = every[:use]
+
+        def fn(q):
+            for i, (o, l, r) in enumerate(terms):
+                last = q.matmul(ap(o), ap(l), ap(r), start is None or (start and i == 0), stop is None or (stop and i == len(terms) - 1))
+            return last
+        return op("P", fn, [x for t in every for x in t[1:]], [terms[0][0]], 64 * len(every), tag="mg" + terms[-1][2][0], **k)
 
     def gat(o, win, off, other, f):
         return op("V", lambda q: q.tensor_tensor(ap(o), ap(win).indirect(ap(off)), ap(other), f), [win, off, other], [o],
                   GATHER * (o[2] - o[1]))
 
-    def iota(o, pat, base, cm):
-        if SCRATCH[o[0]][2] == "int32":
-            return op("G", lambda q: q.iota(ap(o), pat, base, cm), [], [o], o[2] - o[1])
-        return op("G", lambda q: q.iota(ap(o), pat, base, cm, allow_small_or_imprecise_dtypes=True), [], [o], o[2] - o[1])
+    def pick(e, o, win, off, m, v):
+        fn = ((lambda q: q.activation(ap(o), ap(win).indirect(ap(off)), F.Identity, bias=v, scale=m)) if e == "S" else
+              (lambda q: q.tensor_scalar(ap(o), ap(win).indirect(ap(off)), m, v, A.mult, A.add)))
+        return op(e, fn, [win, off], [o], GATHER * (o[2] - o[1]))
 
-    def load(e, o, src, sem, lat):
-        k = op(e, lambda q: q.dma_start(ap(o), src), [], [o, ("turn" + e, 0, 1)], 0, sem=sem, lat=lat)
-        ops[k]["deps"] = {d: True for d in ops[k]["deps"]}
+    def iota(o, pat, base, cm, lo=0, hi=128):
+        n = (o[2] - o[1]) // (o[3] if len(o) > 3 else 1)
+        if SCRATCH[o[0]][2] == "int32":
+            return op("G", lambda q: q.iota(ap(o), pat, base, cm), [], [o], n)
+        return op("G", lambda q: q.iota(ap(o, lo, hi), pat, base, cm, allow_small_or_imprecise_dtypes=True), [], [o], n)
+
+    def mark_at(o, i, pat, base, v):
+        return op("G", lambda q: q.affine_select(ap(o), ap(i), pat, A.not_equal, v, base, 1), [i], [o], 150)
+
+    def dma(e, fn, rd, wr, sem, lat):
+        k = op(e, fn, rd, wr + [("turn" + e, 0, 1)], 0, sem=sem, lat=lat)
+        ops[k]["deps"] = {d: ops[d]["e"] == e or ops[d]["sem"] == sem for d in ops[k]["deps"]}
+
+    def load(e, o, src, s, c0, c1, sem, lat, half=0):
+        for h in range(2):
+            dma(e, lambda q, h=h: q.dma_start(ap(o, 64 * h, 64 * h + 64), src[64 * s:64 * s + 64, c0 + h * half:c1 + h * half]),
+                [], [(o[0] + "h%d" % h, o[1], o[2])], sem, lat)
+            touch.setdefault(o[0], []).append((len(ops) - 1, (o[0], o[1], o[2], True)))
 
     def C(k):
         return ("col", k, k + 1)
 
-    def X(c):
-        return ("xw", OFF + CUT[c], OFF + CUT[c + 1])
+    def X(s, c):
+        return ("xw%d" % s, OFF + CUT[c], OFF + CUT[c + 1])
 
-    def K(nm, c, sh=0, more=0):
-        return (nm, CUT[c] + sh, CUT[c + 1] + sh + more)
+    def K(nm, s, c, sh=0, more=0):
+        return (nm + str(s), CUT[c] + sh, CUT[c + 1] + sh + more)
 
-    def PS(b, c):
-        return ("ps%d" % b, 0, CUT[c + 1] - CUT[c])
+    def KK(nm, s, c):
+        return (nm + str(s), CUT[c] // 16, CUT[c + 1] // 16)
 
-    def KK(c, n=1):
-        return (CUT[c] // 16, CUT[c + n] // 16)
+    def M(nm):
+        return (nm, 0, 128)
 
-    def fold(src, sel, c0, c1):
-        return [((sel, 15 - s, 143 - s), (src, CUT[c0] + s, CUT[c1], 16)) for s in range(16)]
+    def EW(b):
+        return ("ew", 128 * b, 128 * b + 128)
 
-    load("S", ("kcs", 0, 4), T.kc[:, :], "lk", 2200)
-    load("Y", X(0), T.x[:, CUT[0]:CUT[1]], "lx0", 2300)
-    load("Y", ("was", 0, 4), T.wa[:, :], "lw", 2200)
-    load("Y", ("hls", 0, 8), T.hl[:, :], "lh", 2200)
-    for c in range(1, NC):
-        load("Y", X(c), T.x[:, CUT[c]:CUT[c + 1]], "lx%d" % c, 2300 + 300 * c)
-    load("Y", ("tab", 0, W), T.inv[:, :], "lt", 7000)
-    iota(("pi", 0, 1), [[1, 1]], 0, 1)
+    def fold(src, sel, a=0, b=Q):
+        return [((sel, 15 - k, 143 - k), (src, a + k, b, 16)) for k in range(16)]
+
+    load("S", ("kcs", 0, 4), T.kc, 0, 0, 4, "lk0", 2200)
+    load("Y", K("rr", 0, 0), T.x, 0, CUT[0], CUT[1], "lx0", 2300, Q)
+    load("S", ("was", 0, 4), T.wa, 0, 0, 4, "lw0", 2200)
+    load("Y", K("rr", 0, 1), T.x, 0, CUT[1], CUT[2], "lx1", 2500, Q)
+    load("Y", ("hls", 0, 8), T.hl, 0, 0, 8, "lh0", 2200)
+    load("S", ("kcs", 16, 20), T.kc, 1, 0, 4, "lk1", 2200)
+    load("S", ("was", 8, 12), T.wa, 1, 0, 4, "lw1", 2200)
+    load("Y", ("hls", 8, 16), T.hl, 1, 0, 8, "lh1", 2200)
+    for c in range(NC):
+        load("Y", K("rr", 1, c), T.x, 1, CUT[c], CUT[c + 1], "lx%d" % (2 + c), 2900 + 300 * c, Q)
+    load("Y", ("tab0", 0, W), T.inv, 0, 0, W, "lt0", 7000)
+    iota(("pi", 0, 8), [[0, 8]], 0, 1)
+    iota(("pi", 8, 16), [[1, 8]], 0, 0)
+    iota(C(6), [[0, 1]], 0, 1)
+    iota(("jt", 0, 64), [[0, 4], [2, 16]], 1, 0)
+    iota(M("g16"), [[16, 8], [0, 16]], 0, 0)
     iota(("mi", 0, 144), [[1, 144]], 0, 0)
-    iota(("g16", 0, 128), [[16, 8], [0, 16]], 0, 0)
-    iota(("cc", 0, KP), [[16, KP]], OFF - 2048, 0)
-    cp(C(0), ("pi", 0, 1))
-    ts(("pi", 1, 2), ("pi", 0, 1), 15, None, A.bitwise_and)
-    cp(C(1), ("pi", 1, 2))
-    tt(C(2), C(0), C(1), A.subtract)
-    ts(C(3), C(1), -DELTA, 15 * DELTA, A.mult, A.add)
+    iota(("cc", 0, KP), [[16, KP]], OFF - 1024, 0)
+    iota(M("no"), [[0, 128]], 0, 0)
+    for h in range(2):
+        iota(("kt", 0, 16 * NK), [[0, 16], [OPEN, NK]], -OPEN * (1 - h) * (rank > 0), 0, 64 * h, 64 * h + 64)
+    iota(("kt", 0, 16 * NK, NK), [[0, 16]], NONE, 0, 0, 64)
+    iota(("rs", 0, 16 * NK), [[0, 16], [32767, NK]], -17000, 0)
+    mark_at(M("ib"), M("no"), [[-1, 128]], 0, 1.0)
+    mark_at(M("sh"), M("no"), [[-1, 128]], 64, 1.0)
+    mark_at(M("up"), M("no"), [[0, 2], [-1, 64]], -64, 1.0)
+    mark_at(M("dn"), M("no"), [[0, 2], [-1, 64]], -64, -1.0)
+    mark_at(M("lu"), M("dn"), [[0, 2], [-1, 64]], 0, 1.0)
+    mark_at(M("nd"), M("dn"), [[0, 2], [-1, 64]], 0, -1.0)
+    ts(("pi", 16, 24), ("pi", 0, 8), 15, None, A.bitwise_and)
+    cp(C(1), ("pi", 16, 17))
+    cp(("of", 0, 16), ("pi", 8, 24))
+    tt(C(2), C(6), C(1), A.subtract)
+    ts(C(3), C(1), -NK * DELTA, (OFF - 16 - NK) * DELTA, A.mult, A.add)
     ts(C(4), C(2), 15.0, None, A.add)
-    ts(C(5), C(2), -0.5, None, A.add)
-    ts(("bm", 0, 128), ("g16", 0, 128), C(2), None, A.is_equal)
-    ts(("jt", 0, 128), ("mi", 0, 128), C(5), 1.0 / 16, A.subtract, A.mult)
-    tt(("jt", 0, 128), ("jt", 0, 128), ("bm", 0, 128), A.mult)
-    ts(("col", 32, 36), ("was", 0, 4), 1.0 / 32768, None, A.mult)
-    ts(("col", 20, 24), ("hls", 0, 4), 65536.0, None, A.add)
-    ts(("col", 8, 12), ("hls", 4, 8), 1.0 / 32768, None, A.mult)
-    for u in range(RU):
-        b = (128 * u, 128 * u + 128)
-        act(("wb",) + b, ("bm", 0, 128), F.Identity, 0.0, C(32 + u))
-        ts(("ek",) + b, ("jt", 0, 128), ("kcs", u, u + 1), 192.0, A.mult, A.add)
-        ts(("yy",) + b, ("jt", 0, 128), ("kcs", u, u + 1), 192.0, A.mult, A.add)
-        tt(("yy",) + b, ("ek",) + b, ("yy",) + b, A.subtract)
-        act(("e1",) + b, ("yy",) + b, F.Sign, 0.0, 1.0)
-    ms(("xw", 0, 16), -512.0)
-    ms(("cap", 0, 1), 2.0)
-    ms(("inc", P, P + 1), DELTA)
-    for nm, v in (("nh", -1.0), ("ib", 1.0), ("ih", 1.0), ("nb", -1.0), ("iw", 512.0)):
-        ts((nm, 0, 128), ("mi", 0, 128), C(0), v, A.is_equal, A.mult)
-    ts(("colc", 0, KP), ("cc", 0, KP), C(1), None, A.add)
-    ts(("sz", 0, 144), ("mi", 0, 144), C(4), 2048.0, A.is_equal, A.mult)
+    ts(M("bm"), M("g16"), C(2), None, A.is_equal)
     ms(("tw", 0, 12), 2.0)
     ms(("tw", 12, 24), 0.0)
     scan(("tw", 24, 36), ("tw", 0, 12), ("tw", 12, 24), 0.5, A.mult, A.add)
+    ts(C(7), C(1), 2.0, 1.0, A.mult, A.add)
+    ts(("tw", 48, 52), ("tw", 24, 28), C(7), None, A.mult)
+    ts(("tw", 52, 56), ("tw", 48, 52), GRID, GRID, A.add, A.subtract)
+    tt(("tw", 56, 60), ("tw", 52, 56), ("tw", 48, 52), A.subtract)
+    red(C(8), ("tw", 56, 60), apply_absolute_value=True)
+    ts(C(9), C(8), 16384.0, None, A.mult)
+    ts(C(10), C(8), -0.5, 1.0, A.mult, A.add)
+    for s in range(2):
+        now[0] = s
+        y, r, a = ("yy", 64 * s, 64 * s + 64), ("ek", 64 * s, 64 * s + 64), 8 * s
+        gat(y, ("kcs", 16 * s, 16 * s + 4), ("of", 0, 4), ("jt", 0, 64), A.mult)
+        ts(r, y, GRID, GRID, A.add, A.subtract)
+        tt(("cw", 64 * s, 64 * s + 64), r, y, A.subtract)
+        ts(("tw", 60 + 4 * s, 64 + 4 * s), ("was", a, a + 4), 1.0 / 8192, None, A.mult)
+        for u in range(RU):
+            gat(EW(2 * u + s), ("cw", 64 * s + 16 * u, 64 * s + 16 * u + 16), ("of", 8, 16), M("bm"), A.mult)
+            if u == 0:
+                ts(EW(15 - s), M("bm"), ("was", a, a + 1), 1.0 / 32768, A.mult, A.mult)
+            else:
+                act(EW(15 - 2 * u - s), M("bm"), F.Identity, 0.0, ("tw", 60 + 4 * s + u, 61 + 4 * s + u))
+        ts(("hi", a, a + 1), ("hls", a, a + 1), C(9), None, A.add)
+        ts(("lo", a + 4, a + 5), ("hls", a + 4, a + 5), 1.0 / 32768, None, A.mult)
+    now[0] = 0
+    act(M("b64"), M("bm"), F.Identity, 0.0, -64.0)
+    p = PS(16)
+    sub([((p[0], 4 * k, 4 * k + 4), M("b64"), ("was", 8 * (k // 2), 8 * (k // 2) + 4)) for k in range(4)], None, None)
+    tt(("hls", 16, 32), p, ("hls", 0, 16), A.add)
+    ts(("hi", 16, 32), ("hls", 16, 32), C(9), None, A.add)
+    ts(("lo", 16, 32), ("hls", 16, 32), 1.0 / 32768, None, A.mult)
+
+    def later(last):
+        first = len(ops)
+        load("Y", ("tab1", 0, W), T.inv, 1, 0, W, "lt1", 5600 - FLIGHT)
+        for s in range(2):
+            ops[first + s].update(after=last[s], pre=("sent%d" % s, sum(len(es) for (t, es) in mine)))
+
+    for s in range(2):
+        iota(("xw%d" % s, 0, 16), [[0, 16]], NONE, 0)
+        ms(("cap%d" % s, 0, 1), 2.0)
+        ms(("inc%d" % s, Q, Q + 1), DELTA)
+    for nm, v in (("nh", -1.0), ("ih", 1.0), ("ir", -1023.0 / 1024), ("i4", 4.0), ("r4", -1023.0 / 256)):
+        act(M(nm), M("ib"), F.Identity, 0.0, v)
+    act(M("ns"), M("sh"), F.Identity, 0.0, -1.0)
+    ts(("colc", 0, KP), ("cc", 0, KP), C(1), None, A.add)
+    ts(("sz", 0, 144), ("mi", 0, 144), C(4), 1.0 / DELTA, A.is_equal, A.mult)
     ts(("tw", 36, 48), ("mi", 0, 12), C(1), None, A.is_equal)
     tt(("tw", 36, 48), ("tw", 36, 48), ("tw", 24, 36), A.mult)
-    op("V", lambda q: q.tensor_reduce(ap(C(6)), ap(("tw", 36, 48)), AxisListType.X, A.add), [("tw", 36, 48)], [C(6)], 12)
-    ts(("sV", 0, 144), ("mi", 0, 144), C(4), C(6), A.is_equal, A.mult)
-    act(("sS", 0, 144), ("sV", 0, 144), F.Identity, 0.0, 0.5)
-    act(("sn", 0, 144), ("sV", 0, 144), F.Identity, 0.0, -1.0)
-    for k, v in ((25, -1.0), (36, 2048.0), (27, -127.5), (28, MAGIC), (29, MAGIC - 127.5)):
-        ms(C(k), v)
+    red(C(15), ("tw", 36, 48))
+    ts(C(15), C(15), DELTA, None, A.mult)
+    act(("sv", 0, 144), ("sz", 0, 144), F.Identity, 0.0, C(15))
 
     mine = masks(T, topo, rank)
     come = [(d, len(es)) for d in range(1, HB + 1) if rank - d >= 0 for (t, es) in masks(T, topo, rank - d) if t == rank]
 
-    def evac(e, o, i, k, v, relu=False):
+    def E(k, u, s):
+        return LAST.get((k, u, s), ENG[k])
+
+    def evac(e, o, i, m, v, relu=False):
         if e == "S":
-            return act(o, i, F.Relu if relu else F.Identity, C(k), 1.0)
-        return ts(o, i, v, 0.0, A.add, A.max) if relu else ts(o, i, v, None, A.add)
+            return act(o, i, F.Relu if relu else F.Identity, v, m)
+        return ts(o, i, v, 0.0, A.add, A.max) if relu else ts(o, i, m, v, A.mult, A.add)
 
-    def judge(u, c):
-        b = (128 * u, 128 * u + 128)
-        p0, p1 = PS(SB[c], c), PS(MB[c], c)
-        ts(K("bb", c), X(c), 128.0, 0.5, A.is_ge, A.subtract)
-        mm(p0, [(("wb",) + b, X(c))])
-        ts(K("inc", c), p0, C(8 + u), DELTA, A.is_le, A.max)
-        mm(p1, [(("wb",) + b, X(c)), (("e1",) + b, K("bb", c))])
-        act(K("cap", c, 1), p1, F.Relu, C(20 + u), -32768.0)
+    def judge(u, s, c):
+        e, w, n = EW(2 * u + s), EW(15 - 2 * u - s), CUT[c + 1] - CUT[c]
+        x, a = (X(s, c), 16 + 8 * s + u) if u else (K("rr", s, c), 8 * s)
+        p0, p1 = PS(n), PS(n)
+        ts(K("bb", s, c), x, 16.0 if u else 128.0, 0.5, A.is_ge, A.subtract)
+        mm(p0, [(w, x)])
+        ts(K("inc", s, c), p0, ("lo", a + 4, a + 5), DELTA, A.is_le, A.max)
+        mm(p1, [(w, x)], stop=False)
+        mm(p1, [(e, K("bb", s, c))], start=False)
+        act(K("cap", s, c, 1), p1, F.Relu, ("hi", a, a + 1), -32768.0)
         m = 1 if c == NC - 1 else 0
-        ini = C(3) if c == 0 else ("st", CUT[c] - 1, CUT[c])
-        return scan(K("st", c, 0, m), K("cap", c, 0, m), K("inc", c, 0, m), ini, A.min, A.add)
+        ini = C(3) if c == 0 else ("st%d" % s, CUT[c] - 1, CUT[c])
+        scan(K("st", s, c, 0, m), K("cap", s, c, 0, m), K("inc", s, c, 0, m), ini, A.min, A.add)
 
-    def send(u):
-        s = ("snd", 32 * u, 32 * u + 32)
-        tr = []
+    def summary(u, s):
+        w, o, a = ("xw%d" % s, 0, WIN), ("sx%d" % s, 0, 1), 16 * (2 * u + s)
+        src, tr = ("snd", a, a + 16), []
+        iota((w[0], 16, OFF), [[0, OFF - 16]], OPEN, 0)
+        ts(o, ("st%d" % s, Q, Q + 1), -1.0 / DELTA, float(OFF + Q), A.mult, A.add)
+        op("V", lambda q: q.tensor_copy(ap(src), ap(w).indirect(ap(o))), [w, o], [src], 32)
+        if not mine:
+            return op("G", None, [src], [], 170, sem="")
         for (t, es) in mine:
             rid, pid = topo.addr(T.cores[t], core)
             tr.append(RemoteDMATransfer(dst_ids=[DstId(rid=rid, pnc=pid)], dma_engine_mask=sum(1 << e for e in es),
-                                        remote_sem=T.sem["arr%d" % u], src=ap(s),
-                                        dst=ap(("in%d" % (t - rank), 32 * u, 32 * u + 32))))
-        return op("G", lambda q: q.remote_dma_fused(tr, local_sem=T.sem.sent), [s], [], 200, sem="")
+                                        remote_sem=T.sem["arr%d" % (2 * u + s)], src=ap(src),
+                                        dst=ap(("in%d" % (t - rank), a, a + 16))))
+        return op("G", lambda q: q.remote_dma_fused(tr, local_sem=T.sem["sent" if u else "sent%d" % s]), [src], [], 170, sem="")
 
-    def summary(u):
-        w, o, a = ("xw", 0, OFF + P), ("sx", 0, 1), 32 * u
-        ms(("xw", 16, 32), -1024.0)
-        ts(o, ("st", P, P + 1), -2048.0, float(OFF + P), A.mult, A.add)
-        op("V", lambda q: q.tensor_copy(ap(("snd", a, a + 16)), ap(w).indirect(ap(o))), [w, o], [("snd", a, a + 16)], 32)
-        op("V", lambda q: q.tensor_scalar(ap(("snd", a + 16, a + 32)), ap(w).indirect(ap(o)), 768.0, -4.0, A.add, A.mult),
-           [w, o], [("snd", a + 16, a + 32)], 32)
-        return send(u)
+    def ahead(u, s):
+        for c in range(NC):
+            pq = PS(CUT[c + 1] - CUT[c])
+            mm(pq, [(EW(2 * u + s), K("bb", s, c)), (M("nh"), K("st", s, c))])
+            evac(E("Z", u, s)[c], K("zz", s, c), pq, 1.0, C(10), True)
+        evac(E("U", u, s), ("uu%d" % s, 0, Q), ("xw%d" % s, OFF, OFF + Q), 1024.0, 64.0)
+        pz = PS(KP)
+        mm(pz, [(M("ih"), ("colc", 0, KP))] + fold("zz%d" % s, "sz"))
+        cp(("ix%d" % s, 0, KP), pz)
 
-    def store(c):
-        op("Y", lambda q: q.dma_start(T.y[:, CUT[c]:CUT[c + 1]], ap(X(c))), [X(c)], [], 0, sem="out", lat=2500)
-
-    for c in range(NC):
-        last = judge(0, c)
-    for u in range(RU):
-        b = (128 * u, 128 * u + 128)
-        if mine:
-            last = summary(u)
+    def behind(u, s, last):
+        a, p = 16 * (2 * u + s), PS(16 * NK)
+        own, in1, in2 = (("snd", a, a + 16), ("in1", a, a + 16), ("in2", a, a + 16))
+        col = [(p[0], i, 16 * NK, NK) for i in range(NK)]
+        sub([(p, M("ib"), ("kt", 0, 16 * NK)), (col[0], M("sh"), own)]
+            + [(col[i], M("ns"), own) for i in range(1, NK)], True, not come, 2 + 2 * len(come))
+        k = sub([(col[1], M("up"), in1), (col[2], M("lu"), in1), (col[3], M("up"), in2), (col[4], M("lu"), in2),
+                 (col[3], M("nd"), in1), (col[4], M("nd"), in1)],
+                False, True, (2, 2, 6)[len(come)], pre=("arr%d" % (2 * u + s), sum(n for (d, n) in come)), after=last)
+        if not come:
+            ops[k]["fn"] = None
+        scan(("xw%d" % s, 16, OFF), ("rs", 0, 16 * NK), p, 0.0, A.min, A.max)
+        parts = [(CUT[c], CUT[c + 1]) for c in range(NC)] if CF else [(0, Q)]
+        pc = [PS((y - x) // 16) for (x, y) in parts]
+        if CF:
+            r = PS(KP)
+            mm(r, fold("bb%d" % s, "sv"))
+            evac(E("B", u, s), ("cb%d" % s, 0, KP), r, 1.0, -0.5)
+            for r, (x, y) in zip(pc, parts):
+                mm(r, [(M("ih"), ("cb%d" % s, x // 16, y // 16))], stop=False)
+        else:
+            mm(pc[0], fold("bb%d" % s, "sv"), stop=False)
         for c in range(NC):
-            pq, pu = PS(QB[c], c), PS(UB[c], c)
-            mm(pq, [(("e1",) + b, K("bb", c)), (("nh", 0, 128), K("st", c))])
-            evac(ENG["Z"][c], K("zz", c), pq, 25, -1.0, True)
-            ts(K("nl", c), X(c), 64.0, 0.5, A.is_ge, A.subtract)
-            mm(pu, [(("ib", 0, 128), X(c)), (("iw", 0, 128), K("nl", c))])
-            act(K("uu", c), pu, F.Identity, 0.0, 1.0)
-        mm(("ps2", 0, KP), [(("ih", 0, 128), ("colc", 0, KP))] + fold("zz", "sz", 0, NC))
-        cp(("ix", 0, KP), ("ps2", 0, KP))
-        mm(("ps7", 0, KP), fold("bb", "sV", 0, NC) + fold("nl", "sn", 0, NC))
-        evac("S", ("cb", 0, KP), ("ps7", 0, KP), 36, 2048.0)
-        slot, a = ("xw", 16, 32), 32 * u
-        arr = ("arr%d" % u, sum(n for (d, n) in come))
-        if len(come) == 1:
-            cp(slot, ("in1", a, a + 16), pre=arr, after=last)
-        elif len(come) == 2:
-            tt(("hh", 0, 16), ("in2", a, a + 16), ("in1", a + 16, a + 32), A.min, pre=arr, after=last)
-            tt(slot, ("in1", a, a + 16), ("hh", 0, 16), A.max)
+            gat(K("aa", s, c), ("xw%d" % s, 0, OFF + CUT[c + 1]), KK("ix", s, c), K("uu", s, c), A.max)
+            ts(K("ba", s, c), K("aa", s, c), BAND, BAND + 32, A.add, A.is_equal)
+            ts(K("gr", s, c), K("aa", s, c), WIDE, WIDE + 12288, A.add, A.subtract)
+        for r, (x, y) in zip(pc, parts):
+            mm(r, fold("ba%d" % s, "sv", x, y), start=False)
+            ts(("cx%d" % s, x // 16, y // 16), r, 2048.0 if CF else 2047.5, None, A.add)
+        ia, ir, m, v, b = ("ih", "ir", 0.25, -52.0, -15.875) if u + 1 < RU else ("i4", "r4", 1.0, -144.0, -127.5)
         for c in range(NC):
-            gat(K("aa", c), ("xw", 0, OFF + CUT[c + 1]), ("ix",) + KK(c), K("uu", c), A.max)
-            act(K("ba", c), K("aa", c), F.Sign, C(27), 1.0)
-            if c % 2:
-                kk = KK(c - 1, 2)
-                pc = ("ps%d" % (6 + c // 2), 0, kk[1] - kk[0])
-                mm(pc, [(("ih", 0, 128), ("cb",) + kk)] + fold("ba", "sS", c - 1, c + 1))
-                ts(("cx",) + kk, pc, -0.5, None, A.add)
-        for c in range(NC):
-            pz = PS(ZB[c], c)
-            gat(K("zs", c), ("tab", 0, W), ("cx",) + KK(c), K("aa", c), A.add)
-            evac(ENG["Q"][c], K("rr", c), K("zs", c), 29, MAGIC - 127.5)
-            mm(pz, [(("ih", 0, 128), K("zs", c)), (("nb", 0, 128), K("rr", c))])
-            evac(ENG["X"][c], X(c), pz, 28, MAGIC)
+            pz = PS(CUT[c + 1] - CUT[c])
+            pick(E("T", u, s)[c], K("zs", s, c), ("tab%d" % s, 0, W), KK("cx", s, c), m, v)
+            mm(pz, [(M(ia), K("aa", s, c)), (M(ir), K("gr", s, c))], stop=False)
+            mm(pz, [(M("ib"), K("zs", s, c))], start=False)
+            evac(E("Q", u, s)[c], K("rr", s, c), pz, 1.0, b)
+            tt(X(s, c), pz, K("rr", s, c), A.subtract)
             if u + 1 < RU:
-                last = judge(u + 1, c)
+                judge(u + 1, s, c)
             else:
-                store(c)
+                for hf in range(2):
+                    op("Y", lambda q, hf=hf, c=c: q.dma_start(T.y[64 * s:64 * s + 64, hf * Q + CUT[c]:hf * Q + CUT[c + 1]],
+                                                              ap(X(s, c), 64 * hf, 64 * hf + 64)),
+                       [X(s, c)], [], 0, sem="out", lat=2500)
 
-    kind = (len(mine) > 0, len(come))
-    if kind not in ORDERS:
-        ORDERS[kind] = arrange(ops)
-    count, mark, seen = {}, {}, {e: {} for e in Q}
+    for s in range(2):
+        now[0] = s
+        for c in range(NC):
+            judge(0, s, c)
+        evac(E("C", 0, s), ("xw%d" % s, OFF, OFF + Q), ("rr%d" % s, 0, Q), 0.25, -16.0)
+    for u in range(RU):
+        last = []
+        for s in range(2):
+            now[0] = s
+            last.append(summary(u, s))
+        if u == 0:
+            later(last)
+        for s in range(2):
+            now[0] = s
+            ahead(u, s)
+            behind(u, s, last[s])
+
+    if not ORDERS:
+        ORDERS[0] = arrange(ops)
+    order, banks, users = ORDERS[0]
+    bank.update(banks)
+    total = {}
+    for o in ops:
+        if o["sem"]:
+            total[o["sem"]] = total.get(o["sem"], 0) + 16
+    count, mark, seen, tenant = {}, {}, {e: {} for e in QS}, {}
 
     def wait(e, s, v):
         if seen[e].get(s, 0) < v:
-            Q[e].wait_ge(T.sem[s], v)
+            QS[e].wait_ge(T.sem[s], v)
             seen[e][s] = v
 
-    for (k, t) in ORDERS[kind]:
+    for (k, t) in order:
         o = ops[k]
         e = o["e"]
+        hard = [d for d, soft in o["deps"].items() if not soft]
+        if o["acc"] and tenant.get(bank[o["acc"]]) != o["acc"]:
+            o["bank"] = users.get(tenant.get(bank[o["acc"]]), [])
+            hard += o["bank"]
+            tenant[bank[o["acc"]]] = o["acc"]
+        if o["fn"] is None:
+            continue
         need = {}
-        for d, soft in o["deps"].items():
-            if not soft:
-                s, v = mark[d]
-                need[s] = max(need.get(s, 0), v)
+        for d in [x for d in hard for x in ([d] if ops[d]["fn"] else ops[d]["deps"])]:
+            s, v = mark[d]
+            need[s] = max(need.get(s, 0), v)
+        if e == "G" and o["sem"] is None:
+            need["eG"] = count.get("eG", 0)
         for s, v in need.items():
             wait(e, s, v)
         if o["pre"]:
             wait(e, *o["pre"])
-        ins = o["fn"](Q[e])
-        if o["sem"] != "":
-            s, v = (o["sem"], 16) if o["sem"] else ("e" + e, 1)
-            ins.then_inc(T.sem[s], v)
-            count[s] = count.get(s, 0) + v
-            mark[k] = (s, count[s])
+        ins = o["fn"](QS[e])
+        if o["sem"]:
+            ins.then_inc(T.sem[o["sem"]], 16)
+            mark[k] = (o["sem"], total[o["sem"]])
+        elif o["sem"] is None:
+            ins.then_inc(T.sem["e" + e], 1)
+            count["e" + e] = count.get("e" + e, 0) + 1
+            mark[k] = ("e" + e, count["e" + e])
     if mine:
-        count["sent"] = sum(len(es) for (t, es) in mine) * RU
-    for s, v in count.items():
+        count["sent0"] = count["sent1"] = sum(len(es) for (t, es) in mine)
+        count["sent"] = count["sent0"] * 2 * (RU - 1)
+    for s, v in list(count.items()) + list(total.items()):
         wait("G", s, v)
-    return [(ops[k]["e"], t, ops[k]["c"], ops[k]["name"]) for (k, t) in ORDERS[kind]]
+    return ops, order

@@ -3,13 +3,15 @@ from concourse.mybir import AluOpType as A, AxisListType, ActivationFunctionType
 
 P, W, RU, HB = 1792, 4096, 4, 2
 Q, OFF, WIN = P // 2, 96, 992
-CUT = [0, 480, 896]
+CUTS = {}
+LATE = {(3, 1): [0, 480, 704, 896]}
+FIRST = [0, 480, 896]
 NC, KP = 2, Q // 16
 DELTA, BAND, GRID, WIDE = 1.0 / 1024, 3.0 * 2 ** 27 + 32, 3.0 * 2 ** 27, 3.0 * 2 ** 30
 NONE, OPEN, NK = -16384, -32768, 5
-ENG = {"Z": "SS", "Q": "SS", "U": "S", "T": "SS", "C": "S", "B": "S"}
-LAST = {("T", 3, 1): "SV", ("Q", 3, 1): "SV"}
-TRIES = 6000
+ENG = {"Z": "SS", "Q": "SSSS", "U": "S", "T": "SSSS", "C": "S", "B": "S", "A": "V", "X": "VVVV"}
+LAST = {("T", 3, 1): "SVS", ("Q", 3, 1): "SSV"}
+TRIES = 300
 H, B, S4 = "float16", "bfloat16", "float32"
 
 SCRATCH = {nm: ("sbuf", [128, n], d) for (nms, n, d) in (
@@ -17,21 +19,26 @@ SCRATCH = {nm: ("sbuf", [128, n], d) for (nms, n, d) in (
     ("bb0 bb1 zs0 zs1 ba0 ba1 rr0 rr1", Q, B), ("cap0 cap1", Q + 8, B), ("inc0 inc1 st0 st1", Q + 8, H),
     ("zz0 zz1 gr0 gr1 uu0 uu1 aa0 aa1", Q, H), ("ix0 ix1 cx0 cx1", KP, "uint16"), ("sx0 sx1", 4, "uint16"),
     ("snd in1 in2", 16 * 2 * RU, B),
-    ("pi", 32, "int32"), ("of", 24, "uint16"), ("col", 16, S4), ("mi", 144, S4), ("g16 jt yy ek", 128, S4),
-    ("cc", KP, S4), ("colc cb0 cb1", KP, H), ("cw", 256, B), ("bm b64 ib sh ns up dn lu nd no", 128, B), ("ih nh ir i4 r4", 128, H),
-    ("sz", 144, H), ("sv", 144, B), ("kt rs", 80, B), ("tw", 72, S4), ("ew", 2048, B))
+    ("pi", 32, "int32"), ("of", 24, "uint16"), ("col", 16, S4), ("mi", 144, S4), ("g16 m64 jt yy ek", 128, S4),
+    ("cc", KP, S4), ("colc cb0 cb1", KP, H), ("cw", 256, B), ("bm b64 ib sh ns up dn lu nd", 128, B), ("ih nh ir i4 r4", 128, H),
+    ("sz", 144, H), ("sv sw", 144, B), ("bh nb", 128, B), ("kt rs", 80, B), ("tw", 72, S4), ("ew", 2048, B))
     for nm in nms.split()}
 for _b in range(8):
     SCRATCH["ps%d" % _b] = ("psum", [128, 512], S4)
 SEMAPHORES = (["eV", "eS", "eP", "eG", "lw0", "lk0", "lh0", "lw1", "lk1", "lh1", "lt0", "lt1", "out", "sent", "sent0", "sent1"]
               + ["arr%d" % k for k in range(2 * RU)] + ["lx%d" % c for c in range(2 * NC)])
 
-FAC = 1.08
+FAC = 1.0
 COST = {"V": (55 * FAC, 0.83 * FAC), "S": (130 * FAC, 0.83 * FAC), "P": (30 * FAC, 0.42 * FAC), "G": (150 * FAC, 1.66 * FAC), "Y": (60, 0.0)}
-GATHER, HOP, FLIGHT, LAG, SEED = 1.56, 140, 3550, 3000, 123
-CF = True
+GATHER, HOP, FLIGHT, LAG, SEED = 1.56, 140, 3100, 3000, 8
+FOLD = {}
+WHOLE = False
 SPLIT = 2
 HEAT = 150
+PULL = 0.02
+SAME = 140
+PACES, STEPS, WARM = (1.0, 1.35), 25000, 250
+TAB = (4, 2, 2)
 ORDERS = {}
 
 
@@ -54,7 +61,7 @@ def masks(T, topo, r):
 def arrange(ops):
     n = len(ops)
     eng, cost, acc, lat = [o["e"] for o in ops], [o["c"] for o in ops], [o["acc"] for o in ops], [o["lat"] for o in ops]
-    edges = [(d, k, 0 if soft else HOP + lat[d]) for k, o in enumerate(ops) for d, soft in o["deps"].items()]
+    edges = [(d, k, 0 if soft else (SAME if eng[d] == eng[k] else HOP) + lat[d]) for k, o in enumerate(ops) for d, soft in o["deps"].items()]
     edges += [(o["after"], k, FLIGHT) for k, o in enumerate(ops) if o["after"] is not None]
     users = {}
     for k in range(n):
@@ -95,7 +102,7 @@ def arrange(ops):
         idle, bank = {b: (-1.0, None) for b in range(8)}, {}
         for (t, a) in sorted((at[v[0]], a) for a, v in users.items()):
             b = min(idle, key=lambda b: idle[b][0])
-            if idle[b][0] > t:
+            if idle[b][0] > t + 0.01:
                 return None, (idle[b][1], users[a][0], HOP)
             bank[a] = b
             k = users[a][-1]
@@ -112,7 +119,7 @@ def arrange(ops):
                     break
                 extra.append(e)
                 g = graph(edges + extra)
-            end = max(at[k] + cost[k] + lat[k] for k in range(n))
+            end = max(at[k] + cost[k] + lat[k] for k in range(n)) + PULL * sum(at[k] for k in sends)
             if best is not None and end >= best[0]:
                 break
             best = (end, at, bank)
@@ -120,7 +127,7 @@ def arrange(ops):
             pri = [-(back[k] + cost[k]) for k in range(n)]
         return best
 
-    plain = graph(edges)
+    plain, sends = graph(edges), [k for k in range(n) if ops[k]["sem"] == ""]
     tail = [0.0] * n
     for k in range(n - 1, -1, -1):
         tail[k] = cost[k] + max([w + tail[j] for (j, w) in plain[0][k]] + [lat[k]])
@@ -139,7 +146,95 @@ def arrange(ops):
             cur = got
             if got[0] < best[0]:
                 best = got
-    return sorted(((k, best[1][k]) for k in range(n)), key=lambda v: (v[1], v[0])), best[2], users
+    at = polish(ops, sorted(range(n), key=lambda k: (best[1][k], k)), users)
+    return at, banks(dict(at))[0], users
+
+
+def polish(ops, seq, users):
+    n = len(ops)
+    eng, lat = [o["e"] for o in ops], [o["lat"] for o in ops]
+    costs = [[o["c"] * f if o["e"] != "Y" else o["c"] for o in ops] for f in PACES]
+    pre = [[(d, 0 if soft else (SAME if eng[d] == o["e"] else HOP) + lat[d]) for d, soft in o["deps"].items()] + ([(o["after"], FLIGHT)] if o["after"] is not None else [])
+           for o in ops]
+    direct = [set(d for d, w in p) for p in pre]
+    spans, sends = [(v[0], v[-1]) for v in users.values()], [k for k in range(n) if ops[k]["sem"] == ""]
+
+    def times(seq, cost):
+        end, free, last, why = [0.0] * n, {}, {}, [None] * n
+        for k in seq:
+            e = eng[k]
+            t, y = free.get(e, 0.0), (last.get(e), True)
+            for (d, w) in pre[k]:
+                if end[d] + w > t:
+                    t, y = end[d] + w, (d, False)
+            end[k] = free[e] = t + cost[k]
+            last[e], why[k] = k, y
+        k = max(range(n), key=lambda k: end[k] + lat[k])
+        return end[k] + lat[k], end, why, k
+
+    def fits(end):
+        m = 0
+        for (t, d) in sorted([(end[a] - costs[0][a], 1) for (a, b) in spans] + [(end[b] + HOP, -1) for (a, b) in spans]):
+            m += d
+            if m > 8:
+                return False
+        return True
+
+    def value(seq):
+        got = [times(seq, c) for c in costs]
+        return sum((g[0] + PULL * sum(g[1][k] for k in sends)) / f for g, f in zip(got, PACES)) / len(PACES), got
+
+    def move(seq, a, b):
+        i, j = seq.index(a), seq.index(b)
+        need, take = {b}, []
+        for k in seq[j:i - 1 if i else None:-1]:
+            if k in need:
+                if k == a:
+                    return None
+                take.append(k)
+                need |= direct[k]
+        return seq[:i] + take[::-1] + [k for k in seq[i:j + 1] if k not in need] + seq[j + 1:]
+
+    def defer(seq, a, b):
+        i, j = seq.index(a), seq.index(b)
+        take = {a}
+        for k in seq[i + 1:j + 1]:
+            if direct[k] & take:
+                if k == b:
+                    return None
+                take.add(k)
+        return seq[:i] + [k for k in seq[i:j + 1] if k not in take] + [k for k in seq[i:j + 1] if k in take] + seq[j + 1:]
+
+    cur, got = value(seq)
+    best, x = (cur, seq, got), SEED
+    for it in range(STEPS):
+        x = (x * 1103515245 + 12345) % 2147483648
+        g = got[(x >> 9) % len(PACES)]
+        k, links = g[3], []
+        while k is not None:
+            d, queue = g[2][k]
+            if queue and d is not None and d not in direct[k]:
+                links.append((d, k))
+            k = d
+        x = (x * 1103515245 + 12345) % 2147483648
+        a, b = links[(x >> 8) % len(links)]
+        if (x >> 25) % 2:
+            for m in range((x >> 20) % 4):
+                a = next((k for k in seq[seq.index(a) - 1::-1] if eng[k] == eng[b]), a) if seq.index(a) else a
+            new = move(seq, a, b)
+        else:
+            for m in range((x >> 20) % 4):
+                b = next((k for k in seq[seq.index(b) + 1:] if eng[k] == eng[a]), b)
+            new = defer(seq, a, b)
+        if new is None:
+            continue
+        v, g = value(new)
+        x = (x * 1103515245 + 12345) % 2147483648
+        if v <= cur + WARM * (1 - it / STEPS) * ((x >> 8) % 64) / 64 and fits(g[0][1]):
+            seq, cur, got = sorted(new, key=lambda k: g[0][1][k] - costs[0][k]), v, g
+            if v < best[0]:
+                best = (v, seq, got)
+    return [(k, best[2][0][1][k] - costs[0][k]) for k in best[1]]
 
 
 def rank_program(g, core, T, topo):
@@ -147,7 +242,7 @@ def rank_program(g, core, T, topo):
     if rank is None:
         return
     QS = {"V": g.vector, "S": g.scalar, "P": g.tensor, "G": g, "Y": g.sync}
-    ops, touch, bank, fresh, now = [], {}, {}, [0], [0]
+    ops, touch, bank, fresh, now, CUT = [], {}, {}, [0], [0], list(FIRST)
 
     def ap(r, lo=0, hi=128):
         t = T["ps%d" % bank[r[0]]] if r[0][0] == "@" else T[r[0]]
@@ -248,9 +343,12 @@ def rank_program(g, core, T, topo):
 
     def load(e, o, src, s, c0, c1, sem, lat, half=0):
         for h in range(2):
-            dma(e, lambda q, h=h: q.dma_start(ap(o, 64 * h, 64 * h + 64), src[64 * s:64 * s + 64, c0 + h * half:c1 + h * half]),
+            dma(e[h % len(e)], lambda q, h=h: q.dma_start(ap(o, 64 * h, 64 * h + 64), src[64 * s:64 * s + 64, c0 + h * half:c1 + h * half]),
                 [], [(o[0] + "h%d" % h, o[1], o[2])], sem, lat)
             touch.setdefault(o[0], []).append((len(ops) - 1, (o[0], o[1], o[2], True)))
+
+    def E(k, u, s):
+        return LAST.get((k, u, s), ENG[k])
 
     def C(k):
         return ("col", k, k + 1)
@@ -273,8 +371,8 @@ def rank_program(g, core, T, topo):
     def fold(src, sel, a=0, b=Q):
         return [((sel, 15 - k, 143 - k), (src, a + k, b, 16)) for k in range(16)]
 
-    load("S", ("kcs", 0, 4), T.kc, 0, 0, 4, "lk0", 2200)
-    load("Y", K("rr", 0, 0), T.x, 0, CUT[0], CUT[1], "lx0", 2300, Q)
+    load("SY", ("kcs", 0, 4), T.kc, 0, 0, 4, "lk0", 2200)
+    load("SY", K("rr", 0, 0), T.x, 0, CUT[0], CUT[1], "lx0", 2300, Q)
     load("S", ("was", 0, 4), T.wa, 0, 0, 4, "lw0", 2200)
     load("Y", K("rr", 0, 1), T.x, 0, CUT[1], CUT[2], "lx1", 2500, Q)
     load("Y", ("hls", 0, 8), T.hl, 0, 0, 8, "lh0", 2200)
@@ -283,32 +381,42 @@ def rank_program(g, core, T, topo):
     load("Y", ("hls", 8, 16), T.hl, 1, 0, 8, "lh1", 2200)
     for c in range(NC):
         load("Y", K("rr", 1, c), T.x, 1, CUT[c], CUT[c + 1], "lx%d" % (2 + c), 2900 + 300 * c, Q)
-    load("Y", ("tab0", 0, W), T.inv, 0, 0, W, "lt0", 7000)
+
+    def table(a, b, lat):
+        for k in range(a, b):
+            s, h, c = k // 4, k // 2 % 2, k % 2 * W // 2
+            o = ("tab%d" % s, c, c + W // 2)
+            dma("Y", lambda q, s=s, h=h, c=c, o=o: q.dma_start(ap(o, 64 * h, 64 * h + 64), T.inv[64 * s:64 * s + 64, c:c + W // 2]),
+                [], [("tab%d%d" % (s, h), c, c + W // 2)], "lt%d" % s, lat + 1100 * (k - a + 1))
+            touch.setdefault(o[0], []).append((len(ops) - 1, o + (True,)))
+
+    table(0, TAB[0], 3500)
     iota(("pi", 0, 8), [[0, 8]], 0, 1)
     iota(("pi", 8, 16), [[1, 8]], 0, 0)
-    iota(C(6), [[0, 1]], 0, 1)
+    iota(("col", 11, 14), [[64, 3]], -64, 1)
     iota(("jt", 0, 64), [[0, 4], [2, 16]], 1, 0)
     iota(M("g16"), [[16, 8], [0, 16]], 0, 0)
     iota(("mi", 0, 144), [[1, 144]], 0, 0)
     iota(("cc", 0, KP), [[16, KP]], OFF - 1024, 0)
-    iota(M("no"), [[0, 128]], 0, 0)
+    iota(M("m64"), [[0, 2], [1, 64]], 0, 0)
     for h in range(2):
         iota(("kt", 0, 16 * NK), [[0, 16], [OPEN, NK]], -OPEN * (1 - h) * (rank > 0), 0, 64 * h, 64 * h + 64)
     iota(("kt", 0, 16 * NK, NK), [[0, 16]], NONE, 0, 0, 64)
     iota(("rs", 0, 16 * NK), [[0, 16], [32767, NK]], -17000, 0)
-    mark_at(M("ib"), M("no"), [[-1, 128]], 0, 1.0)
-    mark_at(M("sh"), M("no"), [[-1, 128]], 64, 1.0)
-    mark_at(M("up"), M("no"), [[0, 2], [-1, 64]], -64, 1.0)
-    mark_at(M("dn"), M("no"), [[0, 2], [-1, 64]], -64, -1.0)
+    ts(M("ib"), M("mi"), C(12), None, A.is_equal)
+    ts(M("sh"), M("mi"), C(13), None, A.is_equal)
+    ts(M("up"), M("m64"), C(11), None, A.is_equal)
+    act(M("dn"), M("up"), F.Identity, 0.0, -1.0)
     mark_at(M("lu"), M("dn"), [[0, 2], [-1, 64]], 0, 1.0)
     mark_at(M("nd"), M("dn"), [[0, 2], [-1, 64]], 0, -1.0)
     ts(("pi", 16, 24), ("pi", 0, 8), 15, None, A.bitwise_and)
     cp(C(1), ("pi", 16, 17))
     cp(("of", 0, 16), ("pi", 8, 24))
-    tt(C(2), C(6), C(1), A.subtract)
+    tt(C(2), C(12), C(1), A.subtract)
     ts(C(3), C(1), -NK * DELTA, (OFF - 16 - NK) * DELTA, A.mult, A.add)
     ts(C(4), C(2), 15.0, None, A.add)
     ts(M("bm"), M("g16"), C(2), None, A.is_equal)
+    act(M("bh"), M("bm"), F.Identity, 0.0, 0.5)
     ms(("tw", 0, 12), 2.0)
     ms(("tw", 12, 24), 0.0)
     scan(("tw", 24, 36), ("tw", 0, 12), ("tw", 12, 24), 0.5, A.mult, A.add)
@@ -327,7 +435,8 @@ def rank_program(g, core, T, topo):
         tt(("cw", 64 * s, 64 * s + 64), r, y, A.subtract)
         ts(("tw", 60 + 4 * s, 64 + 4 * s), ("was", a, a + 4), 1.0 / 8192, None, A.mult)
         for u in range(RU):
-            gat(EW(2 * u + s), ("cw", 64 * s + 16 * u, 64 * s + 16 * u + 16), ("of", 8, 16), M("bm"), A.mult)
+            gat(EW(2 * u + s), ("cw", 64 * s + 16 * u, 64 * s + 16 * u + 16), ("of", 8, 16),
+                M("bm" if E("A", u, s) == "V" else "bh"), A.mult)
             if u == 0:
                 ts(EW(15 - s), M("bm"), ("was", a, a + 1), 1.0 / 32768, A.mult, A.mult)
             else:
@@ -343,16 +452,16 @@ def rank_program(g, core, T, topo):
     ts(("lo", 16, 32), ("hls", 16, 32), 1.0 / 32768, None, A.mult)
 
     def later(last):
-        first = len(ops)
-        load("Y", ("tab1", 0, W), T.inv, 1, 0, W, "lt1", 5600 - FLIGHT)
         for s in range(2):
-            ops[first + s].update(after=last[s], pre=("sent%d" % s, sum(len(es) for (t, es) in mine)))
+            first = len(ops)
+            table(sum(TAB[:s + 1]), sum(TAB[:s + 2]), 3400 - FLIGHT)
+            ops[first].update(after=last[s], pre=("sent%d" % s, sum(len(es) for (t, es) in mine)))
 
     for s in range(2):
         iota(("xw%d" % s, 0, 16), [[0, 16]], NONE, 0)
         ms(("cap%d" % s, 0, 1), 2.0)
         ms(("inc%d" % s, Q, Q + 1), DELTA)
-    for nm, v in (("nh", -1.0), ("ih", 1.0), ("ir", -1023.0 / 1024), ("i4", 4.0), ("r4", -1023.0 / 256)):
+    for nm, v in (("nh", -1.0), ("ih", 1.0), ("nb", -1.0), ("ir", -1023.0 / 1024), ("i4", 4.0), ("r4", -1023.0 / 256)):
         act(M(nm), M("ib"), F.Identity, 0.0, v)
     act(M("ns"), M("sh"), F.Identity, 0.0, -1.0)
     ts(("colc", 0, KP), ("cc", 0, KP), C(1), None, A.add)
@@ -362,12 +471,10 @@ def rank_program(g, core, T, topo):
     red(C(15), ("tw", 36, 48))
     ts(C(15), C(15), DELTA, None, A.mult)
     act(("sv", 0, 144), ("sz", 0, 144), F.Identity, 0.0, C(15))
+    act(("sw", 0, 144), ("sv", 0, 144), F.Identity, 0.0, 0.5)
 
     mine = masks(T, topo, rank)
     come = [(d, len(es)) for d in range(1, HB + 1) if rank - d >= 0 for (t, es) in masks(T, topo, rank - d) if t == rank]
-
-    def E(k, u, s):
-        return LAST.get((k, u, s), ENG[k])
 
     def evac(e, o, i, m, v, relu=False):
         if e == "S":
@@ -378,13 +485,16 @@ def rank_program(g, core, T, topo):
         e, w, n = EW(2 * u + s), EW(15 - 2 * u - s), CUT[c + 1] - CUT[c]
         x, a = (X(s, c), 16 + 8 * s + u) if u else (K("rr", s, c), 8 * s)
         p0, p1 = PS(n), PS(n)
-        ts(K("bb", s, c), x, 16.0 if u else 128.0, 0.5, A.is_ge, A.subtract)
+        if E("A", u, s) == "V":
+            ts(K("bb", s, c), x, 16.0 if u else 128.0, 0.5, A.is_ge, A.subtract)
+        else:
+            act(K("bb", s, c), x, F.Sign, -15.875 if u else -127.5, 1.0)
         mm(p0, [(w, x)])
         ts(K("inc", s, c), p0, ("lo", a + 4, a + 5), DELTA, A.is_le, A.max)
         mm(p1, [(w, x)], stop=False)
         mm(p1, [(e, K("bb", s, c))], start=False)
         act(K("cap", s, c, 1), p1, F.Relu, ("hi", a, a + 1), -32768.0)
-        m = 1 if c == NC - 1 else 0
+        m = 1 if c == len(CUT) - 2 else 0
         ini = C(3) if c == 0 else ("st%d" % s, CUT[c] - 1, CUT[c])
         scan(K("st", s, c, 0, m), K("cap", s, c, 0, m), K("inc", s, c, 0, m), ini, A.min, A.add)
 
@@ -404,6 +514,7 @@ def rank_program(g, core, T, topo):
         return op("G", lambda q: q.remote_dma_fused(tr, local_sem=T.sem["sent" if u else "sent%d" % s]), [src], [], 170, sem="")
 
     def ahead(u, s):
+        CUT[:] = FIRST
         for c in range(NC):
             pq = PS(CUT[c + 1] - CUT[c])
             mm(pq, [(EW(2 * u + s), K("bb", s, c)), (M("nh"), K("st", s, c))])
@@ -425,38 +536,51 @@ def rank_program(g, core, T, topo):
         if not come:
             ops[k]["fn"] = None
         scan(("xw%d" % s, 16, OFF), ("rs", 0, 16 * NK), p, 0.0, A.min, A.max)
-        parts = [(CUT[c], CUT[c + 1]) for c in range(NC)] if CF else [(0, Q)]
+        CUT[:] = CUTS.get((u, s), FIRST)
+        chunks = range(len(CUT) - 1)
+        CF = FOLD.get((u, s), True)
+        parts = [(CUT[c], CUT[c + 1]) for c in chunks] if CF else [(0, Q)]
         pc = [PS((y - x) // 16) for (x, y) in parts]
+        sb = "sv" if E("A", u, s) == "V" else "sw"
         if CF:
             r = PS(KP)
-            mm(r, fold("bb%d" % s, "sv"))
+            mm(r, fold("bb%d" % s, sb))
             evac(E("B", u, s), ("cb%d" % s, 0, KP), r, 1.0, -0.5)
             for r, (x, y) in zip(pc, parts):
                 mm(r, [(M("ih"), ("cb%d" % s, x // 16, y // 16))], stop=False)
         else:
-            mm(pc[0], fold("bb%d" % s, "sv"), stop=False)
-        for c in range(NC):
+            mm(pc[0], fold("bb%d" % s, sb), stop=False)
+        for c in chunks:
             gat(K("aa", s, c), ("xw%d" % s, 0, OFF + CUT[c + 1]), KK("ix", s, c), K("uu", s, c), A.max)
             ts(K("ba", s, c), K("aa", s, c), BAND, BAND + 32, A.add, A.is_equal)
-            ts(K("gr", s, c), K("aa", s, c), WIDE, WIDE + 12288, A.add, A.subtract)
+            if not WHOLE:
+                ts(K("gr", s, c), K("aa", s, c), WIDE, WIDE + 12288, A.add, A.subtract)
+        if WHOLE:
+            ts(("gr%d" % s, 0, Q), ("aa%d" % s, 0, Q), WIDE, WIDE + 12288, A.add, A.subtract)
         for r, (x, y) in zip(pc, parts):
             mm(r, fold("ba%d" % s, "sv", x, y), start=False)
             ts(("cx%d" % s, x // 16, y // 16), r, 2048.0 if CF else 2047.5, None, A.add)
         ia, ir, m, v, b = ("ih", "ir", 0.25, -52.0, -15.875) if u + 1 < RU else ("i4", "r4", 1.0, -144.0, -127.5)
-        for c in range(NC):
+        CUT[:] = LATE.get((u, s), CUT)
+        for c in range(len(CUT) - 1):
             pz = PS(CUT[c + 1] - CUT[c])
             pick(E("T", u, s)[c], K("zs", s, c), ("tab%d" % s, 0, W), KK("cx", s, c), m, v)
             mm(pz, [(M(ia), K("aa", s, c)), (M(ir), K("gr", s, c))], stop=False)
             mm(pz, [(M("ib"), K("zs", s, c))], start=False)
             evac(E("Q", u, s)[c], K("rr", s, c), pz, 1.0, b)
-            tt(X(s, c), pz, K("rr", s, c), A.subtract)
+            if E("X", u, s)[c] == "V":
+                tt(X(s, c), pz, K("rr", s, c), A.subtract)
+            else:
+                px = PS(CUT[c + 1] - CUT[c])
+                mm(px, [(M(ia), K("aa", s, c)), (M(ir), K("gr", s, c)), (M("ib"), K("zs", s, c))], stop=False)
+                mm(px, [(M("nb"), K("rr", s, c))], start=False)
+                evac("S", X(s, c), px, 1.0, 0.0)
             if u + 1 < RU:
                 judge(u + 1, s, c)
             else:
                 for hf in range(2):
-                    op("Y", lambda q, hf=hf, c=c: q.dma_start(T.y[64 * s:64 * s + 64, hf * Q + CUT[c]:hf * Q + CUT[c + 1]],
-                                                              ap(X(s, c), 64 * hf, 64 * hf + 64)),
-                       [X(s, c)], [], 0, sem="out", lat=2500)
+                    to, x = T.y[64 * s:64 * s + 64, hf * Q + CUT[c]:hf * Q + CUT[c + 1]], X(s, c)
+                    op("Y", lambda q, hf=hf, to=to, x=x: q.dma_start(to, ap(x, 64 * hf, 64 * hf + 64)), [x], [], 0, sem="out", lat=2500)
 
     for s in range(2):
         now[0] = s

from concourse.bass import DstId, RemoteDMATransfer
from concourse.mybir import AluOpType as A, AxisListType, ActivationFunctionType as F

P, W, RU, HB = 1792, 4096, 4, 2
Q, OFF, WIN = P // 2, 96, 992
CUTS = {}
LATE = {(3, 1): [0, 480, 704, 896]}
FIRST = [0, 480, 896]
NC, KP = 2, Q // 16
DELTA, BAND, GRID, WIDE = 1.0 / 1024, 3.0 * 2 ** 27 + 32, 3.0 * 2 ** 27, 3.0 * 2 ** 30
NONE, OPEN, NK = -16384, -32768, 5
ENG = {"Z": "SS", "Q": "SSSS", "U": "S", "T": "SSSS", "C": "S", "B": "S", "A": "V", "X": "VVVV"}
LAST = {("T", 3, 1): "SVS", ("Q", 3, 1): "SSV"}
TRIES = 300
H, B, S4 = "float16", "bfloat16", "float32"

SCRATCH = {nm: ("sbuf", [128, n], d) for (nms, n, d) in (
    ("xw0 xw1", WIN, B), ("tab0 tab1", W, B), ("was kcs", 32, B), ("hls hi lo", 32, S4),
    ("bb0 bb1 zs0 zs1 ba0 ba1 rr0 rr1", Q, B), ("cap0 cap1", Q + 8, B), ("inc0 inc1 st0 st1", Q + 8, H),
    ("zz0 zz1 gr0 gr1 uu0 uu1 aa0 aa1", Q, H), ("ix0 ix1 cx0 cx1", KP, "uint16"), ("sx0 sx1", 4, "uint16"),
    ("snd in1 in2", 16 * 2 * RU, B),
    ("pi", 32, "int32"), ("of", 24, "uint16"), ("col", 16, S4), ("mi", 144, S4), ("g16 m64 jt yy ek", 128, S4),
    ("cc", KP, S4), ("colc cb0 cb1", KP, H), ("cw", 256, B), ("bm b64 ib sh ns up dn lu nd", 128, B), ("ih nh ir i4 r4", 128, H),
    ("sz", 144, H), ("sv sw", 144, B), ("bh nb", 128, B), ("kt rs", 80, B), ("tw", 72, S4), ("ew", 2048, B))
    for nm in nms.split()}
for _b in range(8):
    SCRATCH["ps%d" % _b] = ("psum", [128, 512], S4)
SEMAPHORES = (["eV", "eS", "eP", "eG", "lw0", "lk0", "lh0", "lw1", "lk1", "lh1", "lt0", "lt1", "out", "sent", "sent0", "sent1"]
              + ["arr%d" % k for k in range(2 * RU)] + ["lx%d" % c for c in range(2 * NC)])

FAC = 1.0
COST = {"V": (55 * FAC, 0.83 * FAC), "S": (130 * FAC, 0.83 * FAC), "P": (30 * FAC, 0.42 * FAC), "G": (150 * FAC, 1.66 * FAC), "Y": (60, 0.0)}
GATHER, HOP, FLIGHT, LAG, SEED = 1.56, 140, 3100, 3000, 8
FOLD = {}
WHOLE = False
SPLIT = 2
HEAT = 150
PULL = 0.02
SAME = 140
PACES, STEPS, WARM = (1.0, 1.35), 25000, 250
TAB = (4, 2, 2)
ORDERS = {}


def masks(T, topo, r):
    dst = [d for d in range(r + 1, r + HB + 1) if d < len(T.cores)]
    es = [topo.engines(T.cores[r], T.cores[d]) for d in dst]
    if len(es) == 1:
        es = [es[0][len(es[0]) // 2:]]
    elif len(es) == 2:
        if es[0] == es[1]:
            n = len(es[0]) // 2
            es = [es[0][:n], es[0][n:]]
        else:
            (a, b) = (0, 1) if len(es[0]) > len(es[1]) else (1, 0)
            es[a] = [e for e in es[a] if e not in es[b]]
            es = [e[:len(e) // SPLIT] for e in es]
    return list(zip(dst, es))


def arrange(ops):
    n = len(ops)
    eng, cost, acc, lat = [o["e"] for o in ops], [o["c"] for o in ops], [o["acc"] for o in ops], [o["lat"] for o in ops]
    edges = [(d, k, 0 if soft else (SAME if eng[d] == eng[k] else HOP) + lat[d]) for k, o in enumerate(ops) for d, soft in o["deps"].items()]
    edges += [(o["after"], k, FLIGHT) for k, o in enumerate(ops) if o["after"] is not None]
    users = {}
    for k in range(n):
        if acc[k]:
            users.setdefault(acc[k], []).append(k)

    def place(pri, nxt, cnt, first):
        left, due, at = list(cnt), list(first), [0.0] * n
        busy = {e: [] for e in COST}
        ready = sorted((-pri[k], k) for k in range(n) if not left[k])
        while ready:
            k = ready.pop()[1]
            t, c, b = due[k], cost[k], busy[eng[k]]
            i = len(b)
            while i and b[i - 1][1] > t:
                i -= 1
            while i < len(b) and b[i][0] < t + c:
                t = max(t, b[i][1])
                i += 1
            b.insert(i, (t, t + c))
            at[k] = t
            for (j, w) in nxt[k]:
                due[j] = max(due[j], t + c + w)
                left[j] -= 1
                if not left[j]:
                    ready.append((-pri[j], j))
                    ready.sort()
        return at

    def graph(es):
        fw, bw = [[] for k in range(n)], [[] for k in range(n)]
        for (a, b, w) in es:
            fw[a].append((b, w))
            bw[b].append((a, w))
        return fw, bw, [len(v) for v in bw], [len(v) for v in fw]

    def banks(at):
        idle, bank = {b: (-1.0, None) for b in range(8)}, {}
        for (t, a) in sorted((at[v[0]], a) for a, v in users.items()):
            b = min(idle, key=lambda b: idle[b][0])
            if idle[b][0] > t + 0.01:
                return None, (idle[b][1], users[a][0], HOP)
            bank[a] = b
            k = users[a][-1]
            idle[b] = (at[k] + cost[k] + HOP, k)
        return bank, None

    def solve(pri, rounds):
        best, extra, g = None, [], plain
        for r in range(rounds):
            while True:
                at = place(pri, g[0], g[2], [0.0] * n)
                bank, e = banks(at)
                if bank:
                    break
                extra.append(e)
                g = graph(edges + extra)
            end = max(at[k] + cost[k] + lat[k] for k in range(n)) + PULL * sum(at[k] for k in sends)
            if best is not None and end >= best[0]:
                break
            best = (end, at, bank)
            back = place([-(at[k] + cost[k]) for k in range(n)], g[1], g[3], lat)
            pri = [-(back[k] + cost[k]) for k in range(n)]
        return best

    plain, sends = graph(edges), [k for k in range(n) if ops[k]["sem"] == ""]
    tail = [0.0] * n
    for k in range(n - 1, -1, -1):
        tail[k] = cost[k] + max([w + tail[j] for (j, w) in plain[0][k]] + [lat[k]])
    best = solve([LAG * ops[k]["set"] - tail[k] for k in range(n)], 8)
    x, cur = SEED, best
    for it in range(TRIES):
        x = (x * 1103515245 + 12345) % 2147483648
        t0, pri, lag = cur[0] * ((x >> 8) % 1000) / 1000.0 - 2000, list(cur[1]), ((x >> 20) % 5 - 2) * 400
        span, amp = (1500, 4000, 9000)[(x >> 12) % 3], (500, 1000, 2000)[(x >> 16) % 3]
        for k in range(n):
            if t0 <= pri[k] <= t0 + span:
                x = (x * 1103515245 + 12345) % 2147483648
                pri[k] += (x >> 8) % amp - amp / 2 + lag * ops[k]["set"]
        got = solve(pri, 3)
        if got[0] <= cur[0] + HEAT * (1 - it / TRIES) * ((x >> 5) % 8) / 8:
            cur = got
            if got[0] < best[0]:
                best = got
    at = polish(ops, sorted(range(n), key=lambda k: (best[1][k], k)), users)
    return at, banks(dict(at))[0], users


def polish(ops, seq, users):
    n = len(ops)
    eng, lat = [o["e"] for o in ops], [o["lat"] for o in ops]
    costs = [[o["c"] * f if o["e"] != "Y" else o["c"] for o in ops] for f in PACES]
    pre = [[(d, 0 if soft else (SAME if eng[d] == o["e"] else HOP) + lat[d]) for d, soft in o["deps"].items()] + ([(o["after"], FLIGHT)] if o["after"] is not None else [])
           for o in ops]
    direct = [set(d for d, w in p) for p in pre]
    spans, sends = [(v[0], v[-1]) for v in users.values()], [k for k in range(n) if ops[k]["sem"] == ""]

    def times(seq, cost):
        end, free, last, why = [0.0] * n, {}, {}, [None] * n
        for k in seq:
            e = eng[k]
            t, y = free.get(e, 0.0), (last.get(e), True)
            for (d, w) in pre[k]:
                if end[d] + w > t:
                    t, y = end[d] + w, (d, False)
            end[k] = free[e] = t + cost[k]
            last[e], why[k] = k, y
        k = max(range(n), key=lambda k: end[k] + lat[k])
        return end[k] + lat[k], end, why, k

    def fits(end):
        m = 0
        for (t, d) in sorted([(end[a] - costs[0][a], 1) for (a, b) in spans] + [(end[b] + HOP, -1) for (a, b) in spans]):
            m += d
            if m > 8:
                return False
        return True

    def value(seq):
        got = [times(seq, c) for c in costs]
        return sum((g[0] + PULL * sum(g[1][k] for k in sends)) / f for g, f in zip(got, PACES)) / len(PACES), got

    def move(seq, a, b):
        i, j = seq.index(a), seq.index(b)
        need, take = {b}, []
        for k in seq[j:i - 1 if i else None:-1]:
            if k in need:
                if k == a:
                    return None
                take.append(k)
                need |= direct[k]
        return seq[:i] + take[::-1] + [k for k in seq[i:j + 1] if k not in need] + seq[j + 1:]

    def defer(seq, a, b):
        i, j = seq.index(a), seq.index(b)
        take = {a}
        for k in seq[i + 1:j + 1]:
            if direct[k] & take:
                if k == b:
                    return None
                take.add(k)
        return seq[:i] + [k for k in seq[i:j + 1] if k not in take] + [k for k in seq[i:j + 1] if k in take] + seq[j + 1:]

    cur, got = value(seq)
    best, x = (cur, seq, got), SEED
    for it in range(STEPS):
        x = (x * 1103515245 + 12345) % 2147483648
        g = got[(x >> 9) % len(PACES)]
        k, links = g[3], []
        while k is not None:
            d, queue = g[2][k]
            if queue and d is not None and d not in direct[k]:
                links.append((d, k))
            k = d
        x = (x * 1103515245 + 12345) % 2147483648
        a, b = links[(x >> 8) % len(links)]
        if (x >> 25) % 2:
            for m in range((x >> 20) % 4):
                a = next((k for k in seq[seq.index(a) - 1::-1] if eng[k] == eng[b]), a) if seq.index(a) else a
            new = move(seq, a, b)
        else:
            for m in range((x >> 20) % 4):
                b = next((k for k in seq[seq.index(b) + 1:] if eng[k] == eng[a]), b)
            new = defer(seq, a, b)
        if new is None:
            continue
        v, g = value(new)
        x = (x * 1103515245 + 12345) % 2147483648
        if v <= cur + WARM * (1 - it / STEPS) * ((x >> 8) % 64) / 64 and fits(g[0][1]):
            seq, cur, got = sorted(new, key=lambda k: g[0][1][k] - costs[0][k]), v, g
            if v < best[0]:
                best = (v, seq, got)
    return [(k, best[2][0][1][k] - costs[0][k]) for k in best[1]]


def rank_program(g, core, T, topo):
    rank = T.rank_of(core)
    if rank is None:
        return
    QS = {"V": g.vector, "S": g.scalar, "P": g.tensor, "G": g, "Y": g.sync}
    ops, touch, bank, fresh, now, CUT = [], {}, {}, [0], [0], list(FIRST)

    def ap(r, lo=0, hi=128):
        t = T["ps%d" % bank[r[0]]] if r[0][0] == "@" else T[r[0]]
        return t[lo:hi, r[1]:r[2]:r[3]] if len(r) > 3 else t[lo:hi, r[1]:r[2]]

    def val(s):
        return ap(s) if isinstance(s, tuple) else s

    def op(e, fn, rd, wr, n, sem=None, pre=None, after=None, lat=0, tag=None):
        acc = [(r[0], 0, 512, True) if r[0][0] == "@" else (r[0], r[1], r[2], False) for r in rd if isinstance(r, tuple)]
        acc += [(r[0], 0, 512, True) if r[0][0] == "@" else (r[0], r[1], r[2], True) for r in wr]
        deps = {}
        for a in acc:
            for (k, b) in touch.get(a[0], []):
                if (a[3] or b[3]) and a[1] < b[2] and b[1] < a[2]:
                    deps[k] = False
        for a in acc:
            old = touch.get(a[0], [])
            if a[3]:
                old = [(k, b) for (k, b) in old if not (a[1] <= b[1] and b[2] <= a[2])]
            touch[a[0]] = old + [(len(ops), a)]
        ps = [a[0] for a in acc if a[0][0] == "@"]
        ops.append({"e": e, "fn": fn, "deps": deps, "c": COST[e][0] + COST[e][1] * n, "n": n, "sem": sem, "pre": pre,
                    "after": after, "lat": lat, "set": now[0], "acc": ps[0] if ps else None,
                    "name": (tag or acc[-1][0]) + "." + str(acc[-1 - (tag is not None)][1] // 440)})
        return len(ops) - 1

    def PS(n):
        fresh[0] += 1
        return ("@%d" % fresh[0], 0, n)

    def two(*rs):
        return all(r[0] == "ew" or (r[0][0] != "@" and SCRATCH[r[0]][2] in (B, H)) for r in rs)

    def ts(o, i, s1, s2, o0, o1=None):
        n = (o[2] - o[1]) * (0.5 if two(o, i) else 1)
        if o1 is None:
            return op("V", lambda q: q.tensor_scalar(ap(o), ap(i), val(s1), None, o0), [i, s1], [o], n)
        return op("V", lambda q: q.tensor_scalar(ap(o), ap(i), val(s1), val(s2), o0, o1), [i, s1, s2], [o], n)

    def tt(o, a, b, f, **k):
        return op("V", lambda q: q.tensor_tensor(ap(o), ap(a), ap(b), f), [a, b], [o],
                  (1 if a[0][0] == "@" else 2) * (o[2] - o[1]), **k)

    def cp(o, i, **k):
        return op("V", lambda q: q.tensor_copy(ap(o), ap(i)), [i], [o], o[2] - o[1], **k)

    def ms(o, v):
        return op("V", lambda q: q.memset(ap(o), v), [], [o], o[2] - o[1])

    def red(o, i, **k):
        return op("V", lambda q: q.tensor_reduce(ap(o), ap(i), AxisListType.X, A.add, **k), [i], [o], i[2] - i[1])

    def scan(o, d0, d1, ini, o0, o1):
        return op("V", lambda q: q.tensor_tensor_scan(ap(o), ap(d0), ap(d1), val(ini), o0, o1), [d0, d1, ini], [o],
                  (o[2] - o[1]) * (0.5 if two(o, d0, d1) else 1))

    def act(o, i, f, bias, scale):
        return op("S", lambda q: q.activation(ap(o), ap(i), f, bias=val(bias), scale=val(scale)), [i, bias, scale], [o], o[2] - o[1])

    def mm(o, pairs, start=True, stop=True):
        def fn(q):
            for k, (l, r) in enumerate(pairs):
                last = q.matmul(ap(o), ap(l), ap(r), start and k == 0, stop and k == len(pairs) - 1)
            return last
        return op("P", fn, [x for p in pairs for x in p], [o], len(pairs) * max(64, o[2] - o[1]), tag="mm" + pairs[-1][1][0])

    def sub(every, start, stop, use=None, **k):
        terms = every[:use]

        def fn(q):
            for i, (o, l, r) in enumerate(terms):
                last = q.matmul(ap(o), ap(l), ap(r), start is None or (start and i == 0), stop is None or (stop and i == len(terms) - 1))
            return last
        return op("P", fn, [x for t in every for x in t[1:]], [terms[0][0]], 64 * len(every), tag="mg" + terms[-1][2][0], **k)

    def gat(o, win, off, other, f):
        return op("V", lambda q: q.tensor_tensor(ap(o), ap(win).indirect(ap(off)), ap(other), f), [win, off, other], [o],
                  GATHER * (o[2] - o[1]))

    def pick(e, o, win, off, m, v):
        fn = ((lambda q: q.activation(ap(o), ap(win).indirect(ap(off)), F.Identity, bias=v, scale=m)) if e == "S" else
              (lambda q: q.tensor_scalar(ap(o), ap(win).indirect(ap(off)), m, v, A.mult, A.add)))
        return op(e, fn, [win, off], [o], GATHER * (o[2] - o[1]))

    def iota(o, pat, base, cm, lo=0, hi=128):
        n = (o[2] - o[1]) // (o[3] if len(o) > 3 else 1)
        if SCRATCH[o[0]][2] == "int32":
            return op("G", lambda q: q.iota(ap(o), pat, base, cm), [], [o], n)
        return op("G", lambda q: q.iota(ap(o, lo, hi), pat, base, cm, allow_small_or_imprecise_dtypes=True), [], [o], n)

    def mark_at(o, i, pat, base, v):
        return op("G", lambda q: q.affine_select(ap(o), ap(i), pat, A.not_equal, v, base, 1), [i], [o], 150)

    def dma(e, fn, rd, wr, sem, lat):
        k = op(e, fn, rd, wr + [("turn" + e, 0, 1)], 0, sem=sem, lat=lat)
        ops[k]["deps"] = {d: ops[d]["e"] == e or ops[d]["sem"] == sem for d in ops[k]["deps"]}

    def load(e, o, src, s, c0, c1, sem, lat, half=0):
        for h in range(2):
            dma(e[h % len(e)], lambda q, h=h: q.dma_start(ap(o, 64 * h, 64 * h + 64), src[64 * s:64 * s + 64, c0 + h * half:c1 + h * half]),
                [], [(o[0] + "h%d" % h, o[1], o[2])], sem, lat)
            touch.setdefault(o[0], []).append((len(ops) - 1, (o[0], o[1], o[2], True)))

    def E(k, u, s):
        return LAST.get((k, u, s), ENG[k])

    def C(k):
        return ("col", k, k + 1)

    def X(s, c):
        return ("xw%d" % s, OFF + CUT[c], OFF + CUT[c + 1])

    def K(nm, s, c, sh=0, more=0):
        return (nm + str(s), CUT[c] + sh, CUT[c + 1] + sh + more)

    def KK(nm, s, c):
        return (nm + str(s), CUT[c] // 16, CUT[c + 1] // 16)

    def M(nm):
        return (nm, 0, 128)

    def EW(b):
        return ("ew", 128 * b, 128 * b + 128)

    def fold(src, sel, a=0, b=Q):
        return [((sel, 15 - k, 143 - k), (src, a + k, b, 16)) for k in range(16)]

    load("SY", ("kcs", 0, 4), T.kc, 0, 0, 4, "lk0", 2200)
    load("SY", K("rr", 0, 0), T.x, 0, CUT[0], CUT[1], "lx0", 2300, Q)
    load("S", ("was", 0, 4), T.wa, 0, 0, 4, "lw0", 2200)
    load("Y", K("rr", 0, 1), T.x, 0, CUT[1], CUT[2], "lx1", 2500, Q)
    load("Y", ("hls", 0, 8), T.hl, 0, 0, 8, "lh0", 2200)
    load("S", ("kcs", 16, 20), T.kc, 1, 0, 4, "lk1", 2200)
    load("S", ("was", 8, 12), T.wa, 1, 0, 4, "lw1", 2200)
    load("Y", ("hls", 8, 16), T.hl, 1, 0, 8, "lh1", 2200)
    for c in range(NC):
        load("Y", K("rr", 1, c), T.x, 1, CUT[c], CUT[c + 1], "lx%d" % (2 + c), 2900 + 300 * c, Q)

    def table(a, b, lat):
        for k in range(a, b):
            s, h, c = k // 4, k // 2 % 2, k % 2 * W // 2
            o = ("tab%d" % s, c, c + W // 2)
            dma("Y", lambda q, s=s, h=h, c=c, o=o: q.dma_start(ap(o, 64 * h, 64 * h + 64), T.inv[64 * s:64 * s + 64, c:c + W // 2]),
                [], [("tab%d%d" % (s, h), c, c + W // 2)], "lt%d" % s, lat + 1100 * (k - a + 1))
            touch.setdefault(o[0], []).append((len(ops) - 1, o + (True,)))

    table(0, TAB[0], 3500)
    iota(("pi", 0, 8), [[0, 8]], 0, 1)
    iota(("pi", 8, 16), [[1, 8]], 0, 0)
    iota(("col", 11, 14), [[64, 3]], -64, 1)
    iota(("jt", 0, 64), [[0, 4], [2, 16]], 1, 0)
    iota(M("g16"), [[16, 8], [0, 16]], 0, 0)
    iota(("mi", 0, 144), [[1, 144]], 0, 0)
    iota(("cc", 0, KP), [[16, KP]], OFF - 1024, 0)
    iota(M("m64"), [[0, 2], [1, 64]], 0, 0)
    for h in range(2):
        iota(("kt", 0, 16 * NK), [[0, 16], [OPEN, NK]], -OPEN * (1 - h) * (rank > 0), 0, 64 * h, 64 * h + 64)
    iota(("kt", 0, 16 * NK, NK), [[0, 16]], NONE, 0, 0, 64)
    iota(("rs", 0, 16 * NK), [[0, 16], [32767, NK]], -17000, 0)
    ts(M("ib"), M("mi"), C(12), None, A.is_equal)
    ts(M("sh"), M("mi"), C(13), None, A.is_equal)
    ts(M("up"), M("m64"), C(11), None, A.is_equal)
    act(M("dn"), M("up"), F.Identity, 0.0, -1.0)
    mark_at(M("lu"), M("dn"), [[0, 2], [-1, 64]], 0, 1.0)
    mark_at(M("nd"), M("dn"), [[0, 2], [-1, 64]], 0, -1.0)
    ts(("pi", 16, 24), ("pi", 0, 8), 15, None, A.bitwise_and)
    cp(C(1), ("pi", 16, 17))
    cp(("of", 0, 16), ("pi", 8, 24))
    tt(C(2), C(12), C(1), A.subtract)
    ts(C(3), C(1), -NK * DELTA, (OFF - 16 - NK) * DELTA, A.mult, A.add)
    ts(C(4), C(2), 15.0, None, A.add)
    ts(M("bm"), M("g16"), C(2), None, A.is_equal)
    act(M("bh"), M("bm"), F.Identity, 0.0, 0.5)
    ms(("tw", 0, 12), 2.0)
    ms(("tw", 12, 24), 0.0)
    scan(("tw", 24, 36), ("tw", 0, 12), ("tw", 12, 24), 0.5, A.mult, A.add)
    ts(C(7), C(1), 2.0, 1.0, A.mult, A.add)
    ts(("tw", 48, 52), ("tw", 24, 28), C(7), None, A.mult)
    ts(("tw", 52, 56), ("tw", 48, 52), GRID, GRID, A.add, A.subtract)
    tt(("tw", 56, 60), ("tw", 52, 56), ("tw", 48, 52), A.subtract)
    red(C(8), ("tw", 56, 60), apply_absolute_value=True)
    ts(C(9), C(8), 16384.0, None, A.mult)
    ts(C(10), C(8), -0.5, 1.0, A.mult, A.add)
    for s in range(2):
        now[0] = s
        y, r, a = ("yy", 64 * s, 64 * s + 64), ("ek", 64 * s, 64 * s + 64), 8 * s
        gat(y, ("kcs", 16 * s, 16 * s + 4), ("of", 0, 4), ("jt", 0, 64), A.mult)
        ts(r, y, GRID, GRID, A.add, A.subtract)
        tt(("cw", 64 * s, 64 * s + 64), r, y, A.subtract)
        ts(("tw", 60 + 4 * s, 64 + 4 * s), ("was", a, a + 4), 1.0 / 8192, None, A.mult)
        for u in range(RU):
            gat(EW(2 * u + s), ("cw", 64 * s + 16 * u, 64 * s + 16 * u + 16), ("of", 8, 16),
                M("bm" if E("A", u, s) == "V" else "bh"), A.mult)
            if u == 0:
                ts(EW(15 - s), M("bm"), ("was", a, a + 1), 1.0 / 32768, A.mult, A.mult)
            else:
                act(EW(15 - 2 * u - s), M("bm"), F.Identity, 0.0, ("tw", 60 + 4 * s + u, 61 + 4 * s + u))
        ts(("hi", a, a + 1), ("hls", a, a + 1), C(9), None, A.add)
        ts(("lo", a + 4, a + 5), ("hls", a + 4, a + 5), 1.0 / 32768, None, A.mult)
    now[0] = 0
    act(M("b64"), M("bm"), F.Identity, 0.0, -64.0)
    p = PS(16)
    sub([((p[0], 4 * k, 4 * k + 4), M("b64"), ("was", 8 * (k // 2), 8 * (k // 2) + 4)) for k in range(4)], None, None)
    tt(("hls", 16, 32), p, ("hls", 0, 16), A.add)
    ts(("hi", 16, 32), ("hls", 16, 32), C(9), None, A.add)
    ts(("lo", 16, 32), ("hls", 16, 32), 1.0 / 32768, None, A.mult)

    def later(last):
        for s in range(2):
            first = len(ops)
            table(sum(TAB[:s + 1]), sum(TAB[:s + 2]), 3400 - FLIGHT)
            ops[first].update(after=last[s], pre=("sent%d" % s, sum(len(es) for (t, es) in mine)))

    for s in range(2):
        iota(("xw%d" % s, 0, 16), [[0, 16]], NONE, 0)
        ms(("cap%d" % s, 0, 1), 2.0)
        ms(("inc%d" % s, Q, Q + 1), DELTA)
    for nm, v in (("nh", -1.0), ("ih", 1.0), ("nb", -1.0), ("ir", -1023.0 / 1024), ("i4", 4.0), ("r4", -1023.0 / 256)):
        act(M(nm), M("ib"), F.Identity, 0.0, v)
    act(M("ns"), M("sh"), F.Identity, 0.0, -1.0)
    ts(("colc", 0, KP), ("cc", 0, KP), C(1), None, A.add)
    ts(("sz", 0, 144), ("mi", 0, 144), C(4), 1.0 / DELTA, A.is_equal, A.mult)
    ts(("tw", 36, 48), ("mi", 0, 12), C(1), None, A.is_equal)
    tt(("tw", 36, 48), ("tw", 36, 48), ("tw", 24, 36), A.mult)
    red(C(15), ("tw", 36, 48))
    ts(C(15), C(15), DELTA, None, A.mult)
    act(("sv", 0, 144), ("sz", 0, 144), F.Identity, 0.0, C(15))
    act(("sw", 0, 144), ("sv", 0, 144), F.Identity, 0.0, 0.5)

    mine = masks(T, topo, rank)
    come = [(d, len(es)) for d in range(1, HB + 1) if rank - d >= 0 for (t, es) in masks(T, topo, rank - d) if t == rank]

    def evac(e, o, i, m, v, relu=False):
        if e == "S":
            return act(o, i, F.Relu if relu else F.Identity, v, m)
        return ts(o, i, v, 0.0, A.add, A.max) if relu else ts(o, i, m, v, A.mult, A.add)

    def judge(u, s, c):
        e, w, n = EW(2 * u + s), EW(15 - 2 * u - s), CUT[c + 1] - CUT[c]
        x, a = (X(s, c), 16 + 8 * s + u) if u else (K("rr", s, c), 8 * s)
        p0, p1 = PS(n), PS(n)
        if E("A", u, s) == "V":
            ts(K("bb", s, c), x, 16.0 if u else 128.0, 0.5, A.is_ge, A.subtract)
        else:
            act(K("bb", s, c), x, F.Sign, -15.875 if u else -127.5, 1.0)
        mm(p0, [(w, x)])
        ts(K("inc", s, c), p0, ("lo", a + 4, a + 5), DELTA, A.is_le, A.max)
        mm(p1, [(w, x)], stop=False)
        mm(p1, [(e, K("bb", s, c))], start=False)
        act(K("cap", s, c, 1), p1, F.Relu, ("hi", a, a + 1), -32768.0)
        m = 1 if c == len(CUT) - 2 else 0
        ini = C(3) if c == 0 else ("st%d" % s, CUT[c] - 1, CUT[c])
        scan(K("st", s, c, 0, m), K("cap", s, c, 0, m), K("inc", s, c, 0, m), ini, A.min, A.add)

    def summary(u, s):
        w, o, a = ("xw%d" % s, 0, WIN), ("sx%d" % s, 0, 1), 16 * (2 * u + s)
        src, tr = ("snd", a, a + 16), []
        iota((w[0], 16, OFF), [[0, OFF - 16]], OPEN, 0)
        ts(o, ("st%d" % s, Q, Q + 1), -1.0 / DELTA, float(OFF + Q), A.mult, A.add)
        op("V", lambda q: q.tensor_copy(ap(src), ap(w).indirect(ap(o))), [w, o], [src], 32)
        if not mine:
            return op("G", None, [src], [], 170, sem="")
        for (t, es) in mine:
            rid, pid = topo.addr(T.cores[t], core)
            tr.append(RemoteDMATransfer(dst_ids=[DstId(rid=rid, pnc=pid)], dma_engine_mask=sum(1 << e for e in es),
                                        remote_sem=T.sem["arr%d" % (2 * u + s)], src=ap(src),
                                        dst=ap(("in%d" % (t - rank), a, a + 16))))
        return op("G", lambda q: q.remote_dma_fused(tr, local_sem=T.sem["sent" if u else "sent%d" % s]), [src], [], 170, sem="")

    def ahead(u, s):
        CUT[:] = FIRST
        for c in range(NC):
            pq = PS(CUT[c + 1] - CUT[c])
            mm(pq, [(EW(2 * u + s), K("bb", s, c)), (M("nh"), K("st", s, c))])
            evac(E("Z", u, s)[c], K("zz", s, c), pq, 1.0, C(10), True)
        evac(E("U", u, s), ("uu%d" % s, 0, Q), ("xw%d" % s, OFF, OFF + Q), 1024.0, 64.0)
        pz = PS(KP)
        mm(pz, [(M("ih"), ("colc", 0, KP))] + fold("zz%d" % s, "sz"))
        cp(("ix%d" % s, 0, KP), pz)

    def behind(u, s, last):
        a, p = 16 * (2 * u + s), PS(16 * NK)
        own, in1, in2 = (("snd", a, a + 16), ("in1", a, a + 16), ("in2", a, a + 16))
        col = [(p[0], i, 16 * NK, NK) for i in range(NK)]
        sub([(p, M("ib"), ("kt", 0, 16 * NK)), (col[0], M("sh"), own)]
            + [(col[i], M("ns"), own) for i in range(1, NK)], True, not come, 2 + 2 * len(come))
        k = sub([(col[1], M("up"), in1), (col[2], M("lu"), in1), (col[3], M("up"), in2), (col[4], M("lu"), in2),
                 (col[3], M("nd"), in1), (col[4], M("nd"), in1)],
                False, True, (2, 2, 6)[len(come)], pre=("arr%d" % (2 * u + s), sum(n for (d, n) in come)), after=last)
        if not come:
            ops[k]["fn"] = None
        scan(("xw%d" % s, 16, OFF), ("rs", 0, 16 * NK), p, 0.0, A.min, A.max)
        CUT[:] = CUTS.get((u, s), FIRST)
        chunks = range(len(CUT) - 1)
        CF = FOLD.get((u, s), True)
        parts = [(CUT[c], CUT[c + 1]) for c in chunks] if CF else [(0, Q)]
        pc = [PS((y - x) // 16) for (x, y) in parts]
        sb = "sv" if E("A", u, s) == "V" else "sw"
        if CF:
            r = PS(KP)
            mm(r, fold("bb%d" % s, sb))
            evac(E("B", u, s), ("cb%d" % s, 0, KP), r, 1.0, -0.5)
            for r, (x, y) in zip(pc, parts):
                mm(r, [(M("ih"), ("cb%d" % s, x // 16, y // 16))], stop=False)
        else:
            mm(pc[0], fold("bb%d" % s, sb), stop=False)
        for c in chunks:
            gat(K("aa", s, c), ("xw%d" % s, 0, OFF + CUT[c + 1]), KK("ix", s, c), K("uu", s, c), A.max)
            ts(K("ba", s, c), K("aa", s, c), BAND, BAND + 32, A.add, A.is_equal)
            if not WHOLE:
                ts(K("gr", s, c), K("aa", s, c), WIDE, WIDE + 12288, A.add, A.subtract)
        if WHOLE:
            ts(("gr%d" % s, 0, Q), ("aa%d" % s, 0, Q), WIDE, WIDE + 12288, A.add, A.subtract)
        for r, (x, y) in zip(pc, parts):
            mm(r, fold("ba%d" % s, "sv", x, y), start=False)
            ts(("cx%d" % s, x // 16, y // 16), r, 2048.0 if CF else 2047.5, None, A.add)
        ia, ir, m, v, b = ("ih", "ir", 0.25, -52.0, -15.875) if u + 1 < RU else ("i4", "r4", 1.0, -144.0, -127.5)
        CUT[:] = LATE.get((u, s), CUT)
        for c in range(len(CUT) - 1):
            pz = PS(CUT[c + 1] - CUT[c])
            pick(E("T", u, s)[c], K("zs", s, c), ("tab%d" % s, 0, W), KK("cx", s, c), m, v)
            mm(pz, [(M(ia), K("aa", s, c)), (M(ir), K("gr", s, c))], stop=False)
            mm(pz, [(M("ib"), K("zs", s, c))], start=False)
            evac(E("Q", u, s)[c], K("rr", s, c), pz, 1.0, b)
            if E("X", u, s)[c] == "V":
                tt(X(s, c), pz, K("rr", s, c), A.subtract)
            else:
                px = PS(CUT[c + 1] - CUT[c])
                mm(px, [(M(ia), K("aa", s, c)), (M(ir), K("gr", s, c)), (M("ib"), K("zs", s, c))], stop=False)
                mm(px, [(M("nb"), K("rr", s, c))], start=False)
                evac("S", X(s, c), px, 1.0, 0.0)
            if u + 1 < RU:
                judge(u + 1, s, c)
            else:
                for hf in range(2):
                    to, x = T.y[64 * s:64 * s + 64, hf * Q + CUT[c]:hf * Q + CUT[c + 1]], X(s, c)
                    op("Y", lambda q, hf=hf, to=to, x=x: q.dma_start(to, ap(x, 64 * hf, 64 * hf + 64)), [x], [], 0, sem="out", lat=2500)

    for s in range(2):
        now[0] = s
        for c in range(NC):
            judge(0, s, c)
        evac(E("C", 0, s), ("xw%d" % s, OFF, OFF + Q), ("rr%d" % s, 0, Q), 0.25, -16.0)
    for u in range(RU):
        last = []
        for s in range(2):
            now[0] = s
            last.append(summary(u, s))
        if u == 0:
            later(last)
        for s in range(2):
            now[0] = s
            ahead(u, s)
            behind(u, s, last[s])

    if not ORDERS:
        ORDERS[0] = arrange(ops)
    order, banks, users = ORDERS[0]
    bank.update(banks)
    total = {}
    for o in ops:
        if o["sem"]:
            total[o["sem"]] = total.get(o["sem"], 0) + 16
    count, mark, seen, tenant = {}, {}, {e: {} for e in QS}, {}

    def wait(e, s, v):
        if seen[e].get(s, 0) < v:
            QS[e].wait_ge(T.sem[s], v)
            seen[e][s] = v

    for (k, t) in order:
        o = ops[k]
        e = o["e"]
        hard = [d for d, soft in o["deps"].items() if not soft]
        if o["acc"] and tenant.get(bank[o["acc"]]) != o["acc"]:
            o["bank"] = users.get(tenant.get(bank[o["acc"]]), [])
            hard += o["bank"]
            tenant[bank[o["acc"]]] = o["acc"]
        if o["fn"] is None:
            continue
        need = {}
        for d in [x for d in hard for x in ([d] if ops[d]["fn"] else ops[d]["deps"])]:
            s, v = mark[d]
            need[s] = max(need.get(s, 0), v)
        if e == "G" and o["sem"] is None:
            need["eG"] = count.get("eG", 0)
        for s, v in need.items():
            wait(e, s, v)
        if o["pre"]:
            wait(e, *o["pre"])
        ins = o["fn"](QS[e])
        if o["sem"]:
            ins.then_inc(T.sem[o["sem"]], 16)
            mark[k] = (o["sem"], total[o["sem"]])
        elif o["sem"] is None:
            ins.then_inc(T.sem["e" + e], 1)
            count["e" + e] = count.get("e" + e, 0) + 1
            mark[k] = ("e" + e, count["e" + e])
    if mine:
        count["sent0"] = count["sent1"] = sum(len(es) for (t, es) in mine)
        count["sent"] = count["sent0"] * 2 * (RU - 1)
    for s, v in list(count.items()) + list(total.items()):
        wait("G", s, v)
    return ops, order
